import numpy as np
import ml_dtypes


def mxq(x, axis, fmt="e4m3"):
    dtype, down = {"e4m3": (ml_dtypes.float8_e4m3fn, 7), "e5m2": (ml_dtypes.float8_e5m2, 14)}[fmt]
    v = np.moveaxis(np.asarray(x, np.float32).astype(ml_dtypes.bfloat16).astype(np.float64), axis, -1)
    blocks = v.reshape(v.shape[:-1] + (-1, 32))
    amax = np.abs(blocks).max(-1, keepdims=True)
    byte = np.maximum(np.where(amax > 0, np.frexp(amax)[1] - 1 + 127, 0) - down, 1)
    scale = np.exp2(byte - 127.0)
    codes = (blocks / scale).astype(np.float32).astype(dtype).astype(np.float64)
    return np.moveaxis((codes * scale).reshape(v.shape), -1, axis)


WIDE = False


def mx_kscale(k):
    if not WIDE:
        return np.ones(k)
    levels = np.array([10, -10, 5, -5, 0])
    if k % 512:
        return np.exp2(np.random.permutation(np.resize(levels, k // 32))).repeat(32)
    a = np.empty((k // 512, 16))
    for p in range(k // 512):
        a[p, :8] = np.random.permutation(np.resize(levels, 8))
        for g in range(8):
            far = levels[np.abs(levels - a[p, g]) >= 10]
            a[p, g + 8] = far[np.random.randint(len(far))]
    return np.exp2(a.ravel()).repeat(32)


BF16 = ml_dtypes.bfloat16


def bf(x):
    return np.asarray(x, np.float32).astype(BF16)


def f64(x):
    return np.asarray(x).astype(np.float64)


E2M1 = np.array([0.0, 0.5, 1.0, 1.5, 2.0, 3.0, 4.0, 6.0, -0.0, -0.5, -1.0, -1.5, -2.0, -3.0, -4.0, -6.0])


def pack_weight(w, fmt):
    k, n = w.shape
    w = f64(bf(w)).reshape(k // 32, 32, n)
    amax = np.abs(w).max(1)
    if fmt == "e4m3":
        byte = np.frexp(amax)[1] - 1 + 127 - 7
    else:
        mant, ex = np.frexp(amax / 6.0)
        byte = np.where(mant > 0.5, ex, ex - 1) + 127
    byte = np.clip(np.where(amax > 0, byte, 1), 1, 254)
    scaled = (w * np.exp2(127.0 - byte)[:, None, :]).reshape(k, n).astype(np.float32)
    by_word = np.ascontiguousarray(scaled.reshape(k // 512, 128, 4, n).transpose(0, 1, 3, 2))
    if fmt == "e4m3":
        words = by_word.astype(ml_dtypes.float8_e4m3fn).view(np.uint8)
    else:
        c = by_word.astype(ml_dtypes.float4_e2m1fn).view(np.uint8) & 0xF
        words = c[..., 0::2] | (c[..., 1::2] << 4)
    return np.ascontiguousarray(words), np.ascontiguousarray(byte.astype(np.uint8).reshape(k // 512, 16, n))


def unpack_weight(words, scales, fmt):
    g, p, n, _ = words.shape
    if fmt == "e4m3":
        vals = np.ascontiguousarray(words).view(ml_dtypes.float8_e4m3fn).astype(np.float64)
    else:
        nib = np.empty((g, p, n, 4), np.uint8)
        nib[..., 0::2] = words & 0xF
        nib[..., 1::2] = words >> 4
        vals = E2M1[nib]
    vals = vals * np.repeat(np.exp2(scales.astype(np.float64) - 127.0), 8, axis=1)[..., None]
    return vals.transpose(0, 1, 3, 2).reshape(g * 512, n)
def pack4(w):
    words, scales = pack_weight(w, "e2m1")
    return words.reshape(words.shape[0], 128, -1), scales


def unpack4(words, scales):
    return unpack_weight(words.reshape(words.shape[0], 128, -1, 2), scales, "e2m1")


def planes(Y):
    n, m = Y.shape
    b = f64(bf(Y)).reshape(n // 32, 32, m)
    amax = np.abs(b).max(1)
    byte = np.clip(np.where(amax > 0, np.frexp(amax)[1] - 1 + 127 - 7, 1), 1, 254)
    codes = (b * np.exp2(127.0 - byte)[:, None, :]).reshape(n, m).astype(np.float32).astype(ml_dtypes.float8_e4m3fn).view(np.uint8)
    words = codes.reshape(n // 512, 128, 4, m).transpose(0, 1, 3, 2)
    return np.ascontiguousarray(words), np.ascontiguousarray(byte.astype(np.uint8).reshape(n // 512, 16, m))


C, J, N, E, P = 4, 512, 1536, 1024, 512

def setup_inputs():
    s = mx_kscale(N)
    t = mx_kscale(E)
    f = np.random.uniform(0.1, 0.5, (C, J, 1))
    count = np.random.binomial(2, f, (C, J, N)) + 0.1 * np.random.randn(C, J, N)
    geno = (count - 2 * f) / np.sqrt(2 * f * (1 - f))
    u = np.random.randn(C, N, E) / np.sqrt(N)
    u = u / s[None, :, None] * t[None, None, :]
    traits = 1.5 * np.random.randn(C, E, P) / np.sqrt(E) / t[None, :, None]
    u_words, u_scales = pack4(u.reshape(C * N, E))
    t_words, t_scales = pack4(traits.reshape(C * E, P))
    return {
        "geno": bf(geno * s),
        "u_words": u_words, "u_scales": u_scales,
        "comp_var": bf(np.exp(0.8 * np.random.randn(C, E))),
        "noise_var": bf(np.random.uniform(0.5, 1.0, C)),
        "t_words": t_words, "t_scales": t_scales,
        "snp_scale": bf(np.exp(0.3 * np.random.randn(C, J))),
        "z_other": bf(0.5 * np.random.randn(C, J, P)),
        "trait_scale": bf(np.exp(0.8 * np.random.randn(P))),
    }

def reference(geno, u_words, u_scales, comp_var, noise_var, t_words, t_scales, snp_scale, z_other, trait_scale):
    u = unpack4(u_words, u_scales).reshape(C, N, E)
    traits = unpack4(t_words, t_scales).reshape(C, E, P)
    r = mxq(f64(geno), 2, "e4m3") @ u
    h = r / (f64(comp_var)[:, None, :] + f64(noise_var)[:, None, None])
    score = mxq(h, 2, "e4m3") @ traits
    y = (score * f64(snp_scale)[:, :, None] + f64(z_other)) * f64(trait_scale)
    Y = y.reshape(C * J, P).T
    words, scales = planes(Y)
    return y, words, scales

@@ -1,0 +1,382 @@
+from contextlib import ExitStack
+
+import concourse.mybir as mybir
+from concourse.masks import make_identity
+
+C, J, N, E, T = 4, 512, 1536, 1024, 512
+FLOPS = 2 * C * J * (N * E + E * T)
+
+F32 = mybir.dt.float32
+BF16 = mybir.dt.bfloat16
+I32 = mybir.dt.int32
+U32 = mybir.dt.uint32
+U8 = mybir.dt.uint8
+FP8X4 = mybir.dt.float8_e4m3fn_x4
+FP4X4 = mybir.dt.float4_e2m1fn_x4
+ALU = mybir.AluOpType
+
+P = 128
+KP = 512
+G1 = N // KP
+G2 = E // KP
+JT = J // P
+TILES = C * JT
+
+
+def tile_grouped_association_scores_k7_kernel(
+    tc, geno, u_words, u_scales, comp_var, noise_var, t_words, t_scales,
+    snp_scale, z_other, trait_scale, out_0, out_1, out_2,
+):
+    nc = tc.nc
+    with ExitStack() as ctx:
+        keep = ctx.enter_context(tc.tile_pool(name="keep", bufs=1))
+        work = ctx.enter_context(tc.tile_pool(name="work", bufs=2))
+        ypool = ctx.enter_context(tc.tile_pool(name="ypool", bufs=6))
+        psum = ctx.enter_context(tc.psum_pool(name="psum", bufs=1))
+        ctx.enter_context(tc.manual_schedule())
+
+        def kept(name, shape, dtype):
+            return keep.tile(shape, dtype, name=name, tag=name, align_bytes=64)
+
+        def worked(name, shape, dtype, bufs=2):
+            return work.tile(shape, dtype, name=name, tag=name, align_bytes=64, bufs=bufs)
+
+        def bank(name, shape, dtype, bufs=1):
+            return psum.tile(shape, dtype, name=name, tag=name, bufs=bufs)
+
+        ident = kept("ident", [P, P], F32)
+        ident_bf = kept("ident_bf", [P, P], BF16)
+        var_rows = kept("var_rows", [P, P], BF16)
+        gain_rows = kept("gain_rows", [P, P], BF16)
+        noise = kept("noise", [P, C], BF16)
+        total_var = kept("total_var", [P, C, 8], F32)
+        inv_var = kept("inv_var", [P, C * 8], F32)
+        gains = kept("gains", [P, TILES + 4], F32)
+        trait_b = kept("trait_b", [P, T], F32)
+        inv_b = [[kept("inv_b%d_%d" % (c, g), [P, KP], F32) for g in range(G2)] for c in range(C)]
+        geno_sb = [kept("geno%d" % i, [P, N], BF16) for i in range(TILES)]
+        u_sb = [kept("u%d" % c, [P, G1, 2 * E], U8) for c in range(C)]
+        t_sb = [kept("t%d" % c, [P, G2, 2 * T], U8) for c in range(C)]
+        z_sb = [kept("z%d" % c, [P, JT, T], BF16) for c in range(C)]
+        u_sc_first = kept("u_sc_first", [P, G1, E], U8)
+        u_sc_rest = kept("u_sc_rest", [P, (C - 1) * G1, E], U8)
+        t_sc = kept("t_sc", [P, C * G2, T], U8)
+        y_codes = [kept("y_codes%d" % c, [P, J], U32) for c in range(C)]
+        y_sc = kept("y_sc", [P, J], U8)
+
+        def zero(tile_ap):
+            nc.vector.memset(tile_ap.rearrange("p g n -> p (g n)").bitcast(I32), 0)
+
+        make_identity(nc, ident[:])
+        nc.vector.memset(var_rows[:], 0.0)
+        zero(u_sc_first[:])
+        zero(t_sc[:])
+        nc.vector.memset(gain_rows[:], 0.0)
+        nc.vector.tensor_copy(out=ident_bf[:], in_=ident[:])
+        zero(u_sc_rest[:])
+
+        def load_geno(i):
+            c, jt = divmod(i, JT)
+            nc.sync.dma_start(out=geno_sb[i][:], in_=geno[c, jt * P:(jt + 1) * P, :])
+
+        def load_words(dst, words, first, count):
+            nc.sync.dma_start(
+                out=dst[:].bitcast(I32),
+                in_=words[first:first + count].rearrange("g p n -> p g n").bitcast(I32),
+            )
+
+        def load_scales(dst, scales, first, count):
+            for q in range(4):
+                nc.sync.dma_start(
+                    out=dst[32 * q:32 * q + 4].bitcast(I32),
+                    in_=scales[first:first + count, 4 * q:4 * q + 4, :].rearrange("g r n -> r g n").bitcast(I32),
+                )
+
+        def load_z(c):
+            nc.sync.dma_start(out=z_sb[c][:], in_=z_other[c].rearrange("(s p) n -> p s n", p=P))
+
+        load_geno(0)
+        nc.sync.dma_start(out=var_rows[0:C * 8, :], in_=comp_var.rearrange("c (b n) -> (c b) n", n=P))
+        nc.sync.dma_start(out=noise[:], in_=noise_var.partition_broadcast(P))
+        load_words(u_sb[0], u_words, 0, G1)
+        load_scales(u_sc_first, u_scales, 0, G1)
+        load_geno(1)
+        load_words(t_sb[0], t_words, 0, G2)
+        load_scales(t_sc, t_scales, 0, C * G2)
+        nc.sync.dma_start(out=gain_rows[0:TILES, :], in_=snp_scale.rearrange("c (b n) -> (c b) n", n=P))
+        nc.sync.dma_start(out=gain_rows[TILES:TILES + 4, :], in_=trait_scale.rearrange("(b n) -> b n", n=P))
+        load_geno(2)
+        load_z(0)
+        load_geno(3)
+        load_scales(u_sc_rest, u_scales, G1, (C - 1) * G1)
+        for c in range(1, C):
+            load_geno(c * JT)
+            load_words(u_sb[c], u_words, c * G1, G1)
+            load_geno(c * JT + 1)
+            load_words(t_sb[c], t_words, c * G2, G2)
+            load_geno(c * JT + 2)
+            load_z(c)
+            load_geno(c * JT + 3)
+
+        st = {}
+
+        def live(i):
+            return 0 <= i < TILES
+
+        def u_scale(c, g, h):
+            if c == 0:
+                return u_sc_first[:, g, h * KP:(h + 1) * KP]
+            return u_sc_rest[:, (c - 1) * G1 + g, h * KP:(h + 1) * KP]
+
+        def turn_geno(i, g, dst):
+            words = geno_sb[i][:].bitcast(F32)
+            for u in range(2):
+                nc.tensor.transpose(dst[:, u, :], words[:, 256 * g + u:256 * (g + 1):2], ident[:])
+
+        def spread(cols, first, dst_view, order):
+            xb = bank("x_spread", [P, 4, P], F32)
+            for b in range(4):
+                nc.tensor.transpose(xb[:, b, :], cols[:, first + b:first + b + 1].to_broadcast([P, P]), ident[:])
+            return lambda: nc.scalar.copy(out=dst_view, in_=order(xb[:].rearrange("p b n -> p (b n)")))
+
+        def pair_order(ap):
+            return ap.rearrange("p (m u i) -> p u m i", u=2, i=2)
+
+        def pair_view(ap):
+            return ap.rearrange("p (u m i) -> p u m i", u=2, i=2)
+
+        def spread_inv(c, g):
+            return spread(inv_var, c * 8 + 4 * g, pair_view(inv_b[c][g][:]), pair_order)
+
+        def make_inv_var():
+            xb = bank("x_spread", [P, P], BF16)
+            nc.tensor.transpose(xb[:], var_rows[:], ident_bf[:])
+            nc.vector.tensor_tensor(
+                out=total_var[:],
+                in0=xb[:, 0:C * 8].rearrange("p (c b) -> p c b", b=8),
+                in1=noise[:].unsqueeze(2).to_broadcast([P, C, 8]),
+                op=ALU.add,
+            )
+            nc.vector.reciprocal(out=inv_var[:], in_=total_var[:].rearrange("p c b -> p (c b)"))
+
+        def make_gains():
+            xb = bank("x_spread", [P, P], BF16)
+            nc.tensor.transpose(xb[:], gain_rows[:], ident_bf[:])
+            nc.scalar.copy(out=gains[:], in_=xb[:, 0:TILES + 4])
+
+        def quantize(src, name, width, bufs=2):
+            codes = worked(name + "_codes", [P, width], U32, bufs)
+            scales = worked(name + "_sc", [P, width], U8, bufs)
+            nc.vector.quantize_mx(out=codes[:].bitcast(FP8X4), scales=scales[:], in_=src[:])
+            return codes, scales
+
+        def words_of(tile_ap, groups):
+            return tile_ap.bitcast(F32).rearrange("p (g j u) -> p g j u", g=groups, u=2)
+
+        def turned(bank_ap):
+            return bank_ap.rearrange("p (g u) j -> p g j u", u=2)
+
+        def transposes(s):
+            gi, hi, yi = s, s - 2, s - 4
+            x0 = x1 = x2 = None
+            if live(gi):
+                x0 = bank("x_geno", [P, 4, P], F32, bufs=2)
+                turn_geno(gi, 0, x0[:, 0:2, :])
+                turn_geno(gi, 1, x0[:, 2:4, :])
+            if live(hi):
+                x1 = bank("x_h", [P, 4, P], F32)
+                for g in range(G2):
+                    words = st["h", hi, g][:].bitcast(F32)
+                    for u in range(2):
+                        nc.tensor.transpose(x1[:, 2 * g + u, :], words[:, u * P:(u + 1) * P], ident[:])
+            if live(gi) or live(yi):
+                x2 = bank("x_mix", [P, 4, P], F32)
+            if live(gi):
+                turn_geno(gi, 2, x2[:, 0:2, :])
+            if live(yi):
+                words = st["y_bf", yi][:].bitcast(F32)
+                for u in range(2):
+                    nc.tensor.transpose(x2[:, 2 + u, :], words[:, u * P:(u + 1) * P], ident[:])
+            if live(gi):
+                st["g01", gi] = worked("g01", [P, 2 * KP], BF16)
+                nc.scalar.copy(out=words_of(st["g01", gi][:], 2), in_=turned(x0[:]))
+            if live(hi):
+                st["ht", hi] = worked("ht", [P, 2 * KP], BF16)
+                nc.scalar.copy(out=words_of(st["ht", hi][:], 2), in_=turned(x1[:]))
+            if live(gi):
+                st["g2", gi] = worked("g2", [P, KP], BF16)
+                nc.scalar.copy(out=words_of(st["g2", gi][:], 1), in_=turned(x2[:, 0:2, :]))
+            if live(yi):
+                st["yt", yi] = worked("yt", [P, KP], BF16)
+                nc.scalar.copy(out=words_of(st["yt", yi][:], 1), in_=turned(x2[:, 2:4, :]))
+
+        def stage1(i, h):
+            c = i // JT
+            acc = bank("r%d" % h, [P, KP], F32)
+            for g in range(G1):
+                codes, scales = st["q01", i] if g < 2 else st["q2", i]
+                cols = slice((g % 2) * P, (g % 2 + 1) * P)
+                nc.tensor.matmul_mx(
+                    out=acc[:],
+                    lhsT=codes[:, cols].bitcast(FP8X4),
+                    lhsT_scale=scales[:, cols],
+                    rhs=u_sb[c][:, g, 2 * h * KP:2 * (h + 1) * KP].bitcast(FP4X4),
+                    rhs_scale=u_scale(c, g, h),
+                    start=(g == 0),
+                    stop=(g == G1 - 1),
+                )
+            st["r", i, h] = acc
+
+        def scale_h(i, h):
+            c = i // JT
+            hb = worked("h%d" % h, [P, KP], BF16)
+            nc.vector.tensor_tensor(
+                out=pair_view(hb[:]), in0=pair_order(st["r", i, h][:]), in1=pair_view(inv_b[c][h][:]), op=ALU.mult
+            )
+            st["h", i, h] = hb
+
+        def stage2(i):
+            c = i // JT
+            acc = bank("d", [P, T], F32)
+            for g in range(G2):
+                codes, scales = st["qh", i, g]
+                nc.tensor.matmul_mx(
+                    out=acc[:],
+                    lhsT=codes.bitcast(FP8X4),
+                    lhsT_scale=scales,
+                    rhs=t_sb[c][:, g, :].bitcast(FP4X4),
+                    rhs_scale=t_sc[:, c * G2 + g, :],
+                    start=(g == 0),
+                    stop=(g == G2 - 1),
+                )
+            st["d", i] = acc
+
+        def join(i):
+            c, jt = divmod(i, JT)
+            joined = worked("joined", [P, T], F32)
+            nc.vector.scalar_tensor_tensor(
+                out=joined[:], in0=st["d", i][:], scalar=gains[:, i:i + 1], in1=z_sb[c][:, jt, :],
+                op0=ALU.mult, op1=ALU.add,
+            )
+            st["joined", i] = joined
+
+        def finish(i):
+            c, jt = divmod(i, JT)
+            y = ypool.tile([P, T], F32, name="y", tag="y", align_bytes=64)
+            nc.vector.tensor_tensor(out=y[:], in0=st["joined", i][:], in1=trait_b[:], op=ALU.mult)
+            nc.sync.dma_start(out=out_0[c, jt * P:(jt + 1) * P, :], in_=y[:])
+            st["y", i] = y
+
+        def round_y(i):
+            y_bf = worked("y_bf", [P, T], BF16)
+            nc.scalar.copy(out=pair_view(y_bf[:]), in_=pair_order(st["y", i][:]))
+            st["y_bf", i] = y_bf
+
+        words_out = out_1[0].rearrange("p m t -> p (m t)").bitcast(I32)
+
+        def quantize_y(i):
+            c, jt = divmod(i, JT)
+            cols = slice(jt * P, (jt + 1) * P)
+            nc.vector.quantize_mx(
+                out=y_codes[c][:, cols].bitcast(FP8X4), scales=y_sc[4 * c:P, cols], in_=st["yt", i][:]
+            )
+            first = None
+            if jt == JT - 1:
+                first = jt if c == C - 1 else 0
+            elif c == C - 1 and jt == JT - 2:
+                first = 0
+            if first is not None:
+                nc.sync.dma_start(
+                    out=words_out[:, c * J + first * P:c * J + (jt + 1) * P],
+                    in_=y_codes[c][:, first * P:(jt + 1) * P].bitcast(I32),
+                )
+            if i == TILES - 1:
+                for q in range(4):
+                    (nc.scalar if q % 2 == 0 else nc.sync).dma_start(
+                        out=out_2[0, 4 * q:4 * q + 4, :].rearrange("r (c j) -> c r j", c=C).bitcast(I32),
+                        in_=y_sc[32 * q:32 * q + 16, :].bitcast(I32),
+                    )
+
+        make_inv_var()
+        transposes(0)
+        for g in range(G2):
+            spread_inv(0, g)()
+        st["q01", 0] = quantize(st["g01", 0], "q01", 2 * P)
+        st["q2", 0] = quantize(st["g2", 0], "q2", P)
+        stage1(0, 0)
+        scale_h(0, 0)
+        stage1(0, 1)
+        transposes(1)
+        st["q01", 1] = quantize(st["g01", 1], "q01", 2 * P)
+        scale_h(0, 1)
+        make_gains()
+        for s in range(2, TILES + 1):
+            transposes(s)
+            c_next, phase = divmod(s + 2, JT)
+            if s == 2:
+                spread(gains, TILES, trait_b[:], lambda ap: ap)()
+            elif 1 <= c_next < C and phase in (1, 2):
+                spread_inv(c_next, phase - 1)()
+            if live(s - 3):
+                join(s - 3)
+            if live(s - 1):
+                st["q2", s - 1] = quantize(st["g2", s - 1], "q2", P)
+            if live(s - 3):
+                finish(s - 3)
+                round_y(s - 3)
+            if live(s):
+                st["q01", s] = quantize(st["g01", s], "q01", 2 * P)
+            if live(s - 2):
+                codes, scales = quantize(st["ht", s - 2], "qh", 2 * P)
+                for g in range(G2):
+                    st["qh", s - 2, g] = codes[:, g * P:(g + 1) * P], scales[:, g * P:(g + 1) * P]
+            if live(s - 1):
+                stage1(s - 1, 0)
+                scale_h(s - 1, 0)
+                stage1(s - 1, 1)
+            if live(s - 4):
+                quantize_y(s - 4)
+            if live(s - 1):
+                scale_h(s - 1, 1)
+            if live(s - 2):
+                stage2(s - 2)
+
+        last = TILES - 1
+
+        def turn_y(i, name, bufs):
+            xb = bank(name, [P, 2, P], F32, bufs=bufs)
+            words = st["y_bf", i][:].bitcast(F32)
+            for u in range(2):
+                nc.tensor.transpose(xb[:, u, :], words[:, u * P:(u + 1) * P], ident[:])
+            st["yt", i] = worked("yt", [P, KP], BF16)
+            nc.scalar.copy(out=words_of(st["yt", i][:], 1), in_=turned(xb[:]))
+
+        halves = []
+        for g, (name, bufs) in enumerate((("x_geno", 2), ("x_h", 1))):
+            xb = bank(name, [P, 2, P], F32, bufs=bufs)
+            words = st["h", last, g][:].bitcast(F32)
+            for u in range(2):
+                nc.tensor.transpose(xb[:, u, :], words[:, u * P:(u + 1) * P], ident[:])
+            half = worked("g2", [P, KP], BF16)
+            nc.scalar.copy(out=words_of(half[:], 1), in_=turned(xb[:]))
+            halves.append(half)
+        turn_y(last - 2, "x_mix", 1)
+        join(last - 1)
+        for g in range(G2):
+            codes, scales = quantize(halves[g], "q2", P)
+            st["qh", last, g] = codes[:], scales[:]
+        stage2(last)
+        finish(last - 1)
+        round_y(last - 1)
+        quantize_y(last - 2)
+        join(last)
+        turn_y(last - 1, "x_geno", 2)
+        y_bf = worked("y_bf", [P, T], BF16)
+        nc.vector.tensor_tensor(
+            out=pair_view(y_bf[:]), in0=pair_order(st["joined", last][:]), in1=pair_order(trait_b[:]), op=ALU.mult
+        )
+        st["y_bf", last] = y_bf
+        turn_y(last, "x_mix", 1)
+        finish(last)
+        quantize_y(last - 1)
+        quantize_y(last)

@@ -21,6 +21,7 @@ G1 = N // KP
 G2 = E // KP
 JT = J // P
 TILES = C * JT
+UNSORTED = 2
 
 
 def tile_grouped_association_scores_k7_kernel(
@@ -101,13 +102,13 @@ def tile_grouped_association_scores_k7_kernel(
         load_words(u_sb[0], u_words, 0, G1)
         load_scales(u_sc_first, u_scales, 0, G1)
         load_geno(1)
-        load_words(t_sb[0], t_words, 0, G2)
-        load_scales(t_sc, t_scales, 0, C * G2)
+        load_geno(2)
         nc.sync.dma_start(out=gain_rows[0:TILES, :], in_=snp_scale.rearrange("c (b n) -> (c b) n", n=P))
         nc.sync.dma_start(out=gain_rows[TILES:TILES + 4, :], in_=trait_scale.rearrange("(b n) -> b n", n=P))
-        load_geno(2)
-        load_z(0)
+        load_words(t_sb[0], t_words, 0, G2)
+        load_scales(t_sc, t_scales, 0, C * G2)
         load_geno(3)
+        load_z(0)
         load_scales(u_sc_rest, u_scales, G1, (C - 1) * G1)
         for c in range(1, C):
             load_geno(c * JT)
@@ -128,16 +129,45 @@ def tile_grouped_association_scores_k7_kernel(
                 return u_sc_first[:, g, h * KP:(h + 1) * KP]
             return u_sc_rest[:, (c - 1) * G1 + g, h * KP:(h + 1) * KP]
 
-        def turn_geno(i, g, dst):
-            words = geno_sb[i][:].bitcast(F32)
-            for u in range(2):
-                nc.tensor.transpose(dst[:, u, :], words[:, 256 * g + u:256 * (g + 1):2], ident[:])
+        def sort_view(dst, src):
+            return (
+                dst.rearrange("p (u b k) -> p b u k", u=2, k=4),
+                src.rearrange("p (b k u) -> p b u k", u=2, k=4),
+            )
 
-        def spread(cols, first, dst_view, order):
-            xb = bank("x_spread", [P, 4, P], F32)
-            for b in range(4):
-                nc.tensor.transpose(xb[:, b, :], cols[:, first + b:first + b + 1].to_broadcast([P, P]), ident[:])
-            return lambda: nc.scalar.copy(out=dst_view, in_=order(xb[:].rearrange("p b n -> p (b n)")))
+        def sort_geno_vector(i):
+            st["s01", i] = worked("s01", [P, 2 * 256], F32)
+            dst, src = sort_view(st["s01", i][:], geno_sb[i][:].bitcast(F32)[:, 0:512])
+            nc.vector.tensor_copy(out=dst, in_=src)
+
+        def sort_geno_scalar(i):
+            st["s2", i] = worked("s2", [P, 256], F32)
+            dst, src = sort_view(st["s2", i][:], geno_sb[i][:].bitcast(F32)[:, 512:768])
+            nc.scalar.copy(out=dst, in_=src)
+
+        def turn_geno(i, g, dst):
+            for u in range(2):
+                if i < UNSORTED:
+                    src = geno_sb[i][:].bitcast(F32)[:, 256 * g + u:256 * (g + 1):2]
+                elif g < 2:
+                    src = st["s01", i][:, 256 * u + P * g:256 * u + P * (g + 1)]
+                else:
+                    src = st["s2", i][:, P * u:P * (u + 1)]
+                nc.tensor.transpose(dst[:, u, :], src, ident[:])
+
+        def spread_turn(jobs, name="x_spread"):
+            xb = bank(name, [P, 4, P], F32)
+            for k, (cols, first, dst, order) in enumerate(jobs):
+                for b in range(2):
+                    nc.tensor.transpose(
+                        xb[:, 2 * k + b, :], cols[:, first + b:first + b + 1].to_broadcast([P, P]), ident[:]
+                    )
+            return xb
+
+        def spread_copy(jobs, xb):
+            for k, (cols, first, dst, order) in enumerate(jobs):
+                src = xb[:, 2 * k:2 * k + 2, :].rearrange("p b n -> p (b n)")
+                nc.scalar.copy(out=dst, in_=order(src))
 
         def pair_order(ap):
             return ap.rearrange("p (m u i) -> p u m i", u=2, i=2)
@@ -145,8 +175,20 @@ def tile_grouped_association_scores_k7_kernel(
         def pair_view(ap):
             return ap.rearrange("p (u m i) -> p u m i", u=2, i=2)
 
-        def spread_inv(c, g):
-            return spread(inv_var, c * 8 + 4 * g, pair_view(inv_b[c][g][:]), pair_order)
+        def inv_job(c, k):
+            g, half = divmod(k, 2)
+            return inv_var, c * 8 + 2 * k, pair_view(inv_b[c][g][:])[:, :, 64 * half:64 * (half + 1), :], pair_order
+
+        def trait_job(k):
+            return gains, TILES + 2 * k, trait_b[:, 256 * k:256 * (k + 1)], lambda ap: ap
+
+        def spread_jobs(s):
+            if s == 2 or s == 4:
+                return [inv_job(1, s - 2), inv_job(1, s - 1)]
+            if s == 3:
+                return [trait_job(0), trait_job(1)]
+            c, k = divmod(s + 3, JT)
+            return [inv_job(c, k)] if c < C else []
 
         def make_inv_var():
             xb = bank("x_spread", [P, P], BF16)
@@ -176,9 +218,9 @@ def tile_grouped_association_scores_k7_kernel(
         def turned(bank_ap):
             return bank_ap.rearrange("p (g u) j -> p g j u", u=2)
 
-        def transposes(s):
-            gi, hi, yi = s, s - 2, s - 4
-            x0 = x1 = x2 = None
+        def transposes(s, jobs):
+            gi, hi, yi = s, s - 2, s - 5
+            x0 = x1 = x2 = xb = None
             if live(gi):
                 x0 = bank("x_geno", [P, 4, P], F32, bufs=2)
                 turn_geno(gi, 0, x0[:, 0:2, :])
@@ -189,6 +231,8 @@ def tile_grouped_association_scores_k7_kernel(
                     words = st["h", hi, g][:].bitcast(F32)
                     for u in range(2):
                         nc.tensor.transpose(x1[:, 2 * g + u, :], words[:, u * P:(u + 1) * P], ident[:])
+            if jobs:
+                xb = spread_turn(jobs)
             if live(gi) or live(yi):
                 x2 = bank("x_mix", [P, 4, P], F32)
             if live(gi):
@@ -197,18 +241,19 @@ def tile_grouped_association_scores_k7_kernel(
                 words = st["y_bf", yi][:].bitcast(F32)
                 for u in range(2):
                     nc.tensor.transpose(x2[:, 2 + u, :], words[:, u * P:(u + 1) * P], ident[:])
-            if live(gi):
-                st["g01", gi] = worked("g01", [P, 2 * KP], BF16)
-                nc.scalar.copy(out=words_of(st["g01", gi][:], 2), in_=turned(x0[:]))
             if live(hi):
                 st["ht", hi] = worked("ht", [P, 2 * KP], BF16)
                 nc.scalar.copy(out=words_of(st["ht", hi][:], 2), in_=turned(x1[:]))
             if live(gi):
+                st["g01", gi] = worked("g01", [P, 2 * KP], BF16)
+                nc.scalar.copy(out=words_of(st["g01", gi][:], 2), in_=turned(x0[:]))
                 st["g2", gi] = worked("g2", [P, KP], BF16)
                 nc.scalar.copy(out=words_of(st["g2", gi][:], 1), in_=turned(x2[:, 0:2, :]))
             if live(yi):
-                st["yt", yi] = worked("yt", [P, KP], BF16)
+                st["yt", yi] = worked("yt", [P, KP], BF16, 4)
                 nc.scalar.copy(out=words_of(st["yt", yi][:], 1), in_=turned(x2[:, 2:4, :]))
+            if jobs:
+                spread_copy(jobs, xb)
 
         def stage1(i, h):
             c = i // JT
@@ -260,10 +305,10 @@ def tile_grouped_association_scores_k7_kernel(
             )
             st["joined", i] = joined
 
-        def finish(i):
+        def finish(i, engine):
             c, jt = divmod(i, JT)
             y = ypool.tile([P, T], F32, name="y", tag="y", align_bytes=64)
-            nc.vector.tensor_tensor(out=y[:], in0=st["joined", i][:], in1=trait_b[:], op=ALU.mult)
+            engine.tensor_tensor(out=y[:], in0=st["joined", i][:], in1=trait_b[:], op=ALU.mult)
             nc.sync.dma_start(out=out_0[c, jt * P:(jt + 1) * P, :], in_=y[:])
             st["y", i] = y
 
@@ -282,8 +327,8 @@ def tile_grouped_association_scores_k7_kernel(
             )
             first = None
             if jt == JT - 1:
-                first = jt if c == C - 1 else 0
-            elif c == C - 1 and jt == JT - 2:
+                first = 2 if c == C - 1 else 0
+            elif c == C - 1 and jt == 1:
                 first = 0
             if first is not None:
                 nc.sync.dma_start(
@@ -298,48 +343,41 @@ def tile_grouped_association_scores_k7_kernel(
                     )
 
         make_inv_var()
-        transposes(0)
+        transposes(0, [])
         for g in range(G2):
-            spread_inv(0, g)()
+            jobs = [inv_job(0, 2 * g), inv_job(0, 2 * g + 1)]
+            spread_copy(jobs, spread_turn(jobs, ("x_spread", "x_h")[g]))
         st["q01", 0] = quantize(st["g01", 0], "q01", 2 * P)
         st["q2", 0] = quantize(st["g2", 0], "q2", P)
         stage1(0, 0)
         scale_h(0, 0)
         stage1(0, 1)
-        transposes(1)
-        st["q01", 1] = quantize(st["g01", 1], "q01", 2 * P)
-        scale_h(0, 1)
+        transposes(1, [])
         make_gains()
+        sort_geno_scalar(2)
+        scale_h(0, 1)
+        sort_geno_vector(2)
         for s in range(2, TILES + 1):
-            transposes(s)
-            c_next, phase = divmod(s + 2, JT)
-            if s == 2:
-                spread(gains, TILES, trait_b[:], lambda ap: ap)()
-            elif 1 <= c_next < C and phase in (1, 2):
-                spread_inv(c_next, phase - 1)()
+            st["q01", s - 1] = quantize(st["g01", s - 1], "q01", 2 * P)
+            st["q2", s - 1] = quantize(st["g2", s - 1], "q2", P)
+            if live(s - 6):
+                quantize_y(s - 6)
+            transposes(s, spread_jobs(s))
+            if live(s - 4):
+                round_y(s - 4)
+            if live(s + 1):
+                sort_geno_vector(s + 1)
+                sort_geno_scalar(s + 1)
+            codes, scales = quantize(st["ht", s - 2], "qh", 2 * P)
+            for g in range(G2):
+                st["qh", s - 2, g] = codes[:, g * P:(g + 1) * P], scales[:, g * P:(g + 1) * P]
             if live(s - 3):
                 join(s - 3)
-            if live(s - 1):
-                st["q2", s - 1] = quantize(st["g2", s - 1], "q2", P)
-            if live(s - 3):
-                finish(s - 3)
-                round_y(s - 3)
-            if live(s):
-                st["q01", s] = quantize(st["g01", s], "q01", 2 * P)
-            if live(s - 2):
-                codes, scales = quantize(st["ht", s - 2], "qh", 2 * P)
-                for g in range(G2):
-                    st["qh", s - 2, g] = codes[:, g * P:(g + 1) * P], scales[:, g * P:(g + 1) * P]
-            if live(s - 1):
-                stage1(s - 1, 0)
-                scale_h(s - 1, 0)
-                stage1(s - 1, 1)
-            if live(s - 4):
-                quantize_y(s - 4)
-            if live(s - 1):
-                scale_h(s - 1, 1)
-            if live(s - 2):
-                stage2(s - 2)
+                finish(s - 3, nc.gpsimd)
+            for h in range(G2):
+                stage1(s - 1, h)
+                scale_h(s - 1, h)
+            stage2(s - 2)
 
         last = TILES - 1
 
@@ -348,7 +386,7 @@ def tile_grouped_association_scores_k7_kernel(
             words = st["y_bf", i][:].bitcast(F32)
             for u in range(2):
                 nc.tensor.transpose(xb[:, u, :], words[:, u * P:(u + 1) * P], ident[:])
-            st["yt", i] = worked("yt", [P, KP], BF16)
+            st["yt", i] = worked("yt", [P, KP], BF16, 4)
             nc.scalar.copy(out=words_of(st["yt", i][:], 1), in_=turned(xb[:]))
 
         halves = []
@@ -360,23 +398,27 @@ def tile_grouped_association_scores_k7_kernel(
             half = worked("g2", [P, KP], BF16)
             nc.scalar.copy(out=words_of(half[:], 1), in_=turned(xb[:]))
             halves.append(half)
-        turn_y(last - 2, "x_mix", 1)
+        turn_y(last - 3, "x_mix", 1)
+        round_y(last - 2)
         join(last - 1)
         for g in range(G2):
             codes, scales = quantize(halves[g], "q2", P)
             st["qh", last, g] = codes[:], scales[:]
         stage2(last)
-        finish(last - 1)
+        finish(last - 1, nc.vector)
         round_y(last - 1)
-        quantize_y(last - 2)
+        quantize_y(last - 4)
+        turn_y(last - 2, "x_mix", 1)
         join(last)
+        quantize_y(last - 3)
         turn_y(last - 1, "x_geno", 2)
-        y_bf = worked("y_bf", [P, T], BF16)
+        y_bf = worked("y_last", [P, T], BF16)
         nc.vector.tensor_tensor(
             out=pair_view(y_bf[:]), in0=pair_order(st["joined", last][:]), in1=pair_order(trait_b[:]), op=ALU.mult
         )
         st["y_bf", last] = y_bf
         turn_y(last, "x_mix", 1)
-        finish(last)
+        finish(last, nc.vector)
+        quantize_y(last - 2)
         quantize_y(last - 1)
         quantize_y(last)

@@ -21,7 +21,8 @@ G1 = N // KP
 G2 = E // KP
 JT = J // P
 TILES = C * JT
-UNSORTED = 2
+UNSORTED = 3
+SORTED = 3
 
 
 def tile_grouped_association_scores_k7_kernel(
@@ -32,7 +33,7 @@ def tile_grouped_association_scores_k7_kernel(
     with ExitStack() as ctx:
         keep = ctx.enter_context(tc.tile_pool(name="keep", bufs=1))
         work = ctx.enter_context(tc.tile_pool(name="work", bufs=2))
-        ypool = ctx.enter_context(tc.tile_pool(name="ypool", bufs=6))
+        ypool = ctx.enter_context(tc.tile_pool(name="ypool", bufs=10))
         psum = ctx.enter_context(tc.psum_pool(name="psum", bufs=1))
         ctx.enter_context(tc.manual_schedule())
 
@@ -135,24 +136,18 @@ def tile_grouped_association_scores_k7_kernel(
                 src.rearrange("p (b k u) -> p b u k", u=2, k=4),
             )
 
-        def sort_geno_vector(i):
-            st["s01", i] = worked("s01", [P, 2 * 256], F32)
-            dst, src = sort_view(st["s01", i][:], geno_sb[i][:].bitcast(F32)[:, 0:512])
-            nc.vector.tensor_copy(out=dst, in_=src)
-
-        def sort_geno_scalar(i):
-            st["s2", i] = worked("s2", [P, 256], F32)
-            dst, src = sort_view(st["s2", i][:], geno_sb[i][:].bitcast(F32)[:, 512:768])
+        def sort_geno(i):
+            st["sorted", i] = worked("sorted", [P, SORTED * 256], F32)
+            dst, src = sort_view(st["sorted", i][:], geno_sb[i][:].bitcast(F32)[:, 0:SORTED * 256])
             nc.scalar.copy(out=dst, in_=src)
 
         def turn_geno(i, g, dst):
             for u in range(2):
-                if i < UNSORTED:
+                if i < UNSORTED or g >= SORTED:
                     src = geno_sb[i][:].bitcast(F32)[:, 256 * g + u:256 * (g + 1):2]
-                elif g < 2:
-                    src = st["s01", i][:, 256 * u + P * g:256 * u + P * (g + 1)]
                 else:
-                    src = st["s2", i][:, P * u:P * (u + 1)]
+                    first = P * (SORTED * u + g)
+                    src = st["sorted", i][:, first:first + P]
                 nc.tensor.transpose(dst[:, u, :], src, ident[:])
 
         def spread_turn(jobs, name="x_spread"):
@@ -183,9 +178,9 @@ def tile_grouped_association_scores_k7_kernel(
             return gains, TILES + 2 * k, trait_b[:, 256 * k:256 * (k + 1)], lambda ap: ap
 
         def spread_jobs(s):
-            if s == 2 or s == 4:
-                return [inv_job(1, s - 2), inv_job(1, s - 1)]
-            if s == 3:
+            if s == 3 or s == 4:
+                return [inv_job(1, 2 * s - 6), inv_job(1, 2 * s - 5)]
+            if s == 2:
                 return [trait_job(0), trait_job(1)]
             c, k = divmod(s + 3, JT)
             return [inv_job(c, k)] if c < C else []
@@ -219,7 +214,7 @@ def tile_grouped_association_scores_k7_kernel(
             return bank_ap.rearrange("p (g u) j -> p g j u", u=2)
 
         def transposes(s, jobs):
-            gi, hi, yi = s, s - 2, s - 5
+            gi, hi, yi = s, s - 2, s - 4
             x0 = x1 = x2 = xb = None
             if live(gi):
                 x0 = bank("x_geno", [P, 4, P], F32, bufs=2)
@@ -247,11 +242,17 @@ def tile_grouped_association_scores_k7_kernel(
             if live(gi):
                 st["g01", gi] = worked("g01", [P, 2 * KP], BF16)
                 nc.scalar.copy(out=words_of(st["g01", gi][:], 2), in_=turned(x0[:]))
-                st["g2", gi] = worked("g2", [P, KP], BF16)
-                nc.scalar.copy(out=words_of(st["g2", gi][:], 1), in_=turned(x2[:, 0:2, :]))
-            if live(yi):
-                st["yt", yi] = worked("yt", [P, KP], BF16, 4)
-                nc.scalar.copy(out=words_of(st["yt", yi][:], 1), in_=turned(x2[:, 2:4, :]))
+            if live(gi) or live(yi):
+                lo, hi2 = (0 if live(gi) else 1), (2 if live(yi) else 1)
+                mix = worked("mix", [P, 2, KP], BF16)
+                nc.scalar.copy(
+                    out=words_of(mix[:, lo:hi2, :].rearrange("p g n -> p (g n)"), hi2 - lo),
+                    in_=turned(x2[:, 2 * lo:2 * hi2, :]),
+                )
+                st["g2", gi] = mix[:, 0, :]
+                st["yt", yi] = mix[:, 1, :]
+            if live(s - 3):
+                round_y(s - 3)
             if jobs:
                 spread_copy(jobs, xb)
 
@@ -354,29 +355,26 @@ def tile_grouped_association_scores_k7_kernel(
         stage1(0, 1)
         transposes(1, [])
         make_gains()
-        sort_geno_scalar(2)
         scale_h(0, 1)
-        sort_geno_vector(2)
         for s in range(2, TILES + 1):
-            st["q01", s - 1] = quantize(st["g01", s - 1], "q01", 2 * P)
-            st["q2", s - 1] = quantize(st["g2", s - 1], "q2", P)
-            if live(s - 6):
-                quantize_y(s - 6)
-            transposes(s, spread_jobs(s))
-            if live(s - 4):
-                round_y(s - 4)
             if live(s + 1):
-                sort_geno_vector(s + 1)
-                sort_geno_scalar(s + 1)
+                sort_geno(s + 1)
+            st["q01", s - 1] = quantize(st["g01", s - 1], "q01", 2 * P)
+            if live(s - 3):
+                join(s - 3)
+            st["q2", s - 1] = quantize(st["g2", s - 1], "q2", P)
+            if live(s - 3):
+                finish(s - 3, nc.vector)
+            transposes(s, spread_jobs(s))
             codes, scales = quantize(st["ht", s - 2], "qh", 2 * P)
             for g in range(G2):
                 st["qh", s - 2, g] = codes[:, g * P:(g + 1) * P], scales[:, g * P:(g + 1) * P]
-            if live(s - 3):
-                join(s - 3)
-                finish(s - 3, nc.gpsimd)
-            for h in range(G2):
-                stage1(s - 1, h)
-                scale_h(s - 1, h)
+            stage1(s - 1, 0)
+            scale_h(s - 1, 0)
+            if live(s - 4):
+                quantize_y(s - 4)
+            stage1(s - 1, 1)
+            scale_h(s - 1, 1)
             stage2(s - 2)
 
         last = TILES - 1
@@ -398,8 +396,7 @@ def tile_grouped_association_scores_k7_kernel(
             half = worked("g2", [P, KP], BF16)
             nc.scalar.copy(out=words_of(half[:], 1), in_=turned(xb[:]))
             halves.append(half)
-        turn_y(last - 3, "x_mix", 1)
-        round_y(last - 2)
+        turn_y(last - 2, "x_mix", 1)
         join(last - 1)
         for g in range(G2):
             codes, scales = quantize(halves[g], "q2", P)
@@ -407,10 +404,8 @@ def tile_grouped_association_scores_k7_kernel(
         stage2(last)
         finish(last - 1, nc.vector)
         round_y(last - 1)
-        quantize_y(last - 4)
-        turn_y(last - 2, "x_mix", 1)
         join(last)
-        quantize_y(last - 3)
+        quantize_y(last - 2)
         turn_y(last - 1, "x_geno", 2)
         y_bf = worked("y_last", [P, T], BF16)
         nc.vector.tensor_tensor(
@@ -419,6 +414,5 @@ def tile_grouped_association_scores_k7_kernel(
         st["y_bf", last] = y_bf
         turn_y(last, "x_mix", 1)
         finish(last, nc.vector)
-        quantize_y(last - 2)
         quantize_y(last - 1)
         quantize_y(last)

@@ -57,12 +57,11 @@ def tile_grouped_association_scores_k7_kernel(
         trait_b = kept("trait_b", [P, T], F32)
         inv_b = [[kept("inv_b%d_%d" % (c, g), [P, KP], F32) for g in range(G2)] for c in range(C)]
         geno_sb = [kept("geno%d" % i, [P, N], BF16) for i in range(TILES)]
-        u_sb = [kept("u%d" % c, [P, G1, 2 * E], U8) for c in range(C)]
+        u_sb = [[kept("u%d_%d" % (c, h), [P, G1, E], U8) for h in range(G2)] for c in range(C)]
         t_sb = [kept("t%d" % c, [P, G2, 2 * T], U8) for c in range(C)]
         z_sb = [kept("z%d" % c, [P, JT, T], BF16) for c in range(C)]
-        u_sc_first = kept("u_sc_first", [P, G1, E], U8)
-        u_sc_rest = kept("u_sc_rest", [P, (C - 1) * G1, E], U8)
-        t_sc = kept("t_sc", [P, C * G2, T], U8)
+        u_sc = [kept("u_sc%d" % c, [P, G1, E], U8) for c in range(C)]
+        t_sc = [kept("t_sc%d" % c, [P, G2, T], U8) for c in range(C)]
         y_codes = [kept("y_codes%d" % c, [P, J], U32) for c in range(C)]
         y_sc = kept("y_sc", [P, J], U8)
 
@@ -71,11 +70,13 @@ def tile_grouped_association_scores_k7_kernel(
 
         make_identity(nc, ident[:])
         nc.vector.memset(var_rows[:], 0.0)
-        zero(u_sc_first[:])
-        zero(t_sc[:])
-        nc.vector.memset(gain_rows[:], 0.0)
+        zero(u_sc[0][:])
         nc.vector.tensor_copy(out=ident_bf[:], in_=ident[:])
-        zero(u_sc_rest[:])
+        zero(t_sc[0][:])
+        nc.vector.memset(gain_rows[:], 0.0)
+        for c in range(1, C):
+            zero(u_sc[c][:])
+            zero(t_sc[c][:])
 
         def load_geno(i):
             c, jt = divmod(i, JT)
@@ -85,6 +86,12 @@ def tile_grouped_association_scores_k7_kernel(
             nc.sync.dma_start(
                 out=dst[:].bitcast(I32),
                 in_=words[first:first + count].rearrange("g p n -> p g n").bitcast(I32),
+            )
+
+        def load_u(c, h):
+            nc.sync.dma_start(
+                out=u_sb[c][h][:].bitcast(I32),
+                in_=u_words[c * G1:(c + 1) * G1, :, h * E:(h + 1) * E].rearrange("g p n -> p g n").bitcast(I32),
             )
 
         def load_scales(dst, scales, first, count):
@@ -98,27 +105,30 @@ def tile_grouped_association_scores_k7_kernel(
             nc.sync.dma_start(out=z_sb[c][:], in_=z_other[c].rearrange("(s p) n -> p s n", p=P))
 
         load_geno(0)
-        nc.sync.dma_start(out=var_rows[0:C * 8, :], in_=comp_var.rearrange("c (b n) -> (c b) n", n=P))
-        nc.sync.dma_start(out=noise[:], in_=noise_var.partition_broadcast(P))
-        load_words(u_sb[0], u_words, 0, G1)
-        load_scales(u_sc_first, u_scales, 0, G1)
+        nc.scalar.dma_start(out=noise[:], in_=noise_var.partition_broadcast(P))
+        nc.scalar.dma_start(out=var_rows[0:C * 8, :], in_=comp_var.rearrange("c (b n) -> (c b) n", n=P))
+        load_u(0, 0)
+        load_scales(u_sc[0], u_scales, 0, G1)
         load_geno(1)
+        load_u(0, 1)
         load_geno(2)
         nc.sync.dma_start(out=gain_rows[0:TILES, :], in_=snp_scale.rearrange("c (b n) -> (c b) n", n=P))
         nc.sync.dma_start(out=gain_rows[TILES:TILES + 4, :], in_=trait_scale.rearrange("(b n) -> b n", n=P))
-        load_words(t_sb[0], t_words, 0, G2)
-        load_scales(t_sc, t_scales, 0, C * G2)
         load_geno(3)
-        load_z(0)
-        load_scales(u_sc_rest, u_scales, G1, (C - 1) * G1)
+        load_words(t_sb[0], t_words, 0, G2)
+        load_scales(t_sc[0], t_scales, 0, G2)
         for c in range(1, C):
             load_geno(c * JT)
-            load_words(u_sb[c], u_words, c * G1, G1)
+            load_z(c - 1)
             load_geno(c * JT + 1)
-            load_words(t_sb[c], t_words, c * G2, G2)
+            load_scales(u_sc[c], u_scales, c * G1, G1)
+            load_scales(t_sc[c], t_scales, c * G2, G2)
+            load_u(c, 0)
+            load_u(c, 1)
             load_geno(c * JT + 2)
-            load_z(c)
+            load_words(t_sb[c], t_words, c * G2, G2)
             load_geno(c * JT + 3)
+        load_z(C - 1)
 
         st = {}
 
@@ -126,9 +136,7 @@ def tile_grouped_association_scores_k7_kernel(
             return 0 <= i < TILES
 
         def u_scale(c, g, h):
-            if c == 0:
-                return u_sc_first[:, g, h * KP:(h + 1) * KP]
-            return u_sc_rest[:, (c - 1) * G1 + g, h * KP:(h + 1) * KP]
+            return u_sc[c][:, g, h * KP:(h + 1) * KP]
 
         def sort_view(dst, src):
             return (
@@ -213,60 +221,72 @@ def tile_grouped_association_scores_k7_kernel(
         def turned(bank_ap):
             return bank_ap.rearrange("p (g u) j -> p g j u", u=2)
 
-        def transposes(s, jobs):
-            gi, hi, yi = s, s - 2, s - 4
-            x0 = x1 = x2 = xb = None
+        def turn_pairs(dst, tile_ap):
+            words = tile_ap.bitcast(F32)
+            for u in range(2):
+                nc.tensor.transpose(dst[:, u, :], words[:, u * P:(u + 1) * P], ident[:])
+
+        def turn_g01(i):
+            if live(i):
+                xb = st["x01", i] = bank("x_geno", [P, 4, P], F32)
+                turn_geno(i, 0, xb[:, 0:2, :])
+                turn_geno(i, 1, xb[:, 2:4, :])
+
+        def copy_g01(i):
+            if live(i):
+                st["g01", i] = worked("g01", [P, 2 * KP], BF16)
+                nc.scalar.copy(out=words_of(st["g01", i][:], 2), in_=turned(st["x01", i][:]))
+
+        def turn_mix(gi, yi):
+            xb = st["xmix"] = bank("x_mix", [P, 4, P], F32)
             if live(gi):
-                x0 = bank("x_geno", [P, 4, P], F32, bufs=2)
-                turn_geno(gi, 0, x0[:, 0:2, :])
-                turn_geno(gi, 1, x0[:, 2:4, :])
-            if live(hi):
-                x1 = bank("x_h", [P, 4, P], F32)
-                for g in range(G2):
-                    words = st["h", hi, g][:].bitcast(F32)
-                    for u in range(2):
-                        nc.tensor.transpose(x1[:, 2 * g + u, :], words[:, u * P:(u + 1) * P], ident[:])
-            if jobs:
-                xb = spread_turn(jobs)
-            if live(gi) or live(yi):
-                x2 = bank("x_mix", [P, 4, P], F32)
-            if live(gi):
-                turn_geno(gi, 2, x2[:, 0:2, :])
+                turn_geno(gi, 2, xb[:, 0:2, :])
             if live(yi):
-                words = st["y_bf", yi][:].bitcast(F32)
-                for u in range(2):
-                    nc.tensor.transpose(x2[:, 2 + u, :], words[:, u * P:(u + 1) * P], ident[:])
-            if live(hi):
-                st["ht", hi] = worked("ht", [P, 2 * KP], BF16)
-                nc.scalar.copy(out=words_of(st["ht", hi][:], 2), in_=turned(x1[:]))
-            if live(gi):
-                st["g01", gi] = worked("g01", [P, 2 * KP], BF16)
-                nc.scalar.copy(out=words_of(st["g01", gi][:], 2), in_=turned(x0[:]))
-            if live(gi) or live(yi):
-                lo, hi2 = (0 if live(gi) else 1), (2 if live(yi) else 1)
-                mix = worked("mix", [P, 2, KP], BF16)
-                nc.scalar.copy(
-                    out=words_of(mix[:, lo:hi2, :].rearrange("p g n -> p (g n)"), hi2 - lo),
-                    in_=turned(x2[:, 2 * lo:2 * hi2, :]),
-                )
-                st["g2", gi] = mix[:, 0, :]
-                st["yt", yi] = mix[:, 1, :]
-            if live(s - 3):
-                round_y(s - 3)
-            if jobs:
-                spread_copy(jobs, xb)
+                turn_pairs(xb[:, 2:4, :], st["y_bf", yi][:])
+
+        def copy_mix(gi, yi):
+            lo, hi = (0 if live(gi) else 1), (2 if live(yi) else 1)
+            mix = worked("mix", [P, 2, KP], BF16)
+            nc.scalar.copy(
+                out=words_of(mix[:, lo:hi, :].rearrange("p g n -> p (g n)"), hi - lo),
+                in_=turned(st["xmix"][:, 2 * lo:2 * hi, :]),
+            )
+            st["g2", gi] = mix[:, 0, :]
+            st["yt", yi] = mix[:, 1, :]
+
+        def turn_h(i):
+            xb = st["xh", i] = bank("x_h", [P, 4, P], F32)
+            for g in range(G2):
+                turn_pairs(xb[:, 2 * g:2 * g + 2, :], st["h", i, g][:])
+
+        def copy_h(i):
+            st["ht", i] = worked("ht", [P, 2 * KP], BF16)
+            nc.scalar.copy(out=words_of(st["ht", i][:], 2), in_=turned(st["xh", i][:]))
+
+        def quantize_h(i):
+            codes, scales = quantize(st["ht", i], "qh", 2 * P)
+            for g in range(G2):
+                st["qh", i, g] = codes[:, g * P:(g + 1) * P], scales[:, g * P:(g + 1) * P]
+
+        def quantize_g01(i):
+            codes, scales = quantize(st["g01", i], "q01", 2 * P)
+            for g in range(2):
+                st["qg", i, g] = codes[:, g * P:(g + 1) * P], scales[:, g * P:(g + 1) * P]
+
+        def quantize_g2(i):
+            codes, scales = quantize(st["g2", i], "q2", P)
+            st["qg", i, 2] = codes[:], scales[:]
 
         def stage1(i, h):
             c = i // JT
             acc = bank("r%d" % h, [P, KP], F32)
             for g in range(G1):
-                codes, scales = st["q01", i] if g < 2 else st["q2", i]
-                cols = slice((g % 2) * P, (g % 2 + 1) * P)
+                codes, scales = st["qg", i, g]
                 nc.tensor.matmul_mx(
                     out=acc[:],
-                    lhsT=codes[:, cols].bitcast(FP8X4),
-                    lhsT_scale=scales[:, cols],
-                    rhs=u_sb[c][:, g, 2 * h * KP:2 * (h + 1) * KP].bitcast(FP4X4),
+                    lhsT=codes.bitcast(FP8X4),
+                    lhsT_scale=scales,
+                    rhs=u_sb[c][h][:, g, :].bitcast(FP4X4),
                     rhs_scale=u_scale(c, g, h),
                     start=(g == 0),
                     stop=(g == G1 - 1),
@@ -281,9 +301,9 @@ def tile_grouped_association_scores_k7_kernel(
             )
             st["h", i, h] = hb
 
-        def stage2(i):
+        def stage2(i, name="d", bufs=1):
             c = i // JT
-            acc = bank("d", [P, T], F32)
+            acc = bank(name, [P, T], F32, bufs=bufs)
             for g in range(G2):
                 codes, scales = st["qh", i, g]
                 nc.tensor.matmul_mx(
@@ -291,7 +311,7 @@ def tile_grouped_association_scores_k7_kernel(
                     lhsT=codes.bitcast(FP8X4),
                     lhsT_scale=scales,
                     rhs=t_sb[c][:, g, :].bitcast(FP4X4),
-                    rhs_scale=t_sc[:, c * G2 + g, :],
+                    rhs_scale=t_sc[c][:, g, :],
                     start=(g == 0),
                     stop=(g == G2 - 1),
                 )
@@ -299,7 +319,7 @@ def tile_grouped_association_scores_k7_kernel(
 
         def join(i):
             c, jt = divmod(i, JT)
-            joined = worked("joined", [P, T], F32)
+            joined = worked("joined", [P, T], F32, 3)
             nc.vector.scalar_tensor_tensor(
                 out=joined[:], in0=st["d", i][:], scalar=gains[:, i:i + 1], in1=z_sb[c][:, jt, :],
                 op0=ALU.mult, op1=ALU.add,
@@ -344,31 +364,69 @@ def tile_grouped_association_scores_k7_kernel(
                     )
 
         make_inv_var()
-        transposes(0, [])
+        first = []
+        for g, name in enumerate(("x_geno", "x_mix", "x_h1")):
+            xa = bank(name, [P, 2, P], F32)
+            turn_geno(0, g, xa)
+            part = worked("first%d" % g, [P, KP], BF16, 1)
+            nc.scalar.copy(out=words_of(part[:], 1), in_=turned(xa[:]))
+            first.append(part)
+        for g in range(G1):
+            codes, scales = quantize(first[g], "qfirst%d" % g, P, 1)
+            st["qg", 0, g] = codes[:], scales[:]
         for g in range(G2):
             jobs = [inv_job(0, 2 * g), inv_job(0, 2 * g + 1)]
             spread_copy(jobs, spread_turn(jobs, ("x_spread", "x_h")[g]))
-        st["q01", 0] = quantize(st["g01", 0], "q01", 2 * P)
-        st["q2", 0] = quantize(st["g2", 0], "q2", P)
         stage1(0, 0)
         scale_h(0, 0)
+        turn_g01(1)
+        turn_mix(1, -1)
+        copy_g01(1)
+        copy_mix(1, -1)
         stage1(0, 1)
-        transposes(1, [])
-        make_gains()
         scale_h(0, 1)
+        make_gains()
+        def turn_half(i, g, dst):
+            turn_pairs(dst, st["h", i, g][:])
+
+        def copy_half(i, g, src):
+            st["half", i, g] = worked("half%d" % g, [P, KP], BF16)
+            nc.scalar.copy(out=words_of(st["half", i, g][:], 1), in_=turned(src))
+
+        def quantize_half(i, g):
+            codes, scales = quantize(st["half", i, g], "qh%d" % g, P)
+            st["qh", i, g] = codes[:], scales[:]
+
         for s in range(2, TILES + 1):
+            jobs = spread_jobs(s)
             if live(s + 1):
                 sort_geno(s + 1)
-            st["q01", s - 1] = quantize(st["g01", s - 1], "q01", 2 * P)
+            quantize_g01(s - 1)
+            if s == TILES:
+                quantize_g2(s - 1)
             if live(s - 3):
                 join(s - 3)
-            st["q2", s - 1] = quantize(st["g2", s - 1], "q2", P)
+            if s < TILES:
+                quantize_g2(s - 1)
             if live(s - 3):
                 finish(s - 3, nc.vector)
-            transposes(s, spread_jobs(s))
-            codes, scales = quantize(st["ht", s - 2], "qh", 2 * P)
-            for g in range(G2):
-                st["qh", s - 2, g] = codes[:, g * P:(g + 1) * P], scales[:, g * P:(g + 1) * P]
+            xa = bank("x_h", [P, 2, P], F32)
+            turn_half(s - 2, 0, xa)
+            turn_g01(s)
+            turn_mix(s, s - 4)
+            xb = spread_turn(jobs) if jobs else None
+            xc = bank("x_h1", [P, 2, P], F32)
+            turn_half(s - 2, 1, xc)
+            copy_half(s - 2, 0, xa[:])
+            copy_g01(s)
+            copy_half(s - 2, 1, xc[:])
+            copy_mix(s, s - 4)
+            if live(s - 3):
+                round_y(s - 3)
+            if jobs:
+                spread_copy(jobs, xb)
+            quantize_half(s - 2, 0)
+            quantize_half(s - 2, 1)
             stage1(s - 1, 0)
             scale_h(s - 1, 0)
             if live(s - 4):
@@ -379,40 +437,35 @@ def tile_grouped_association_scores_k7_kernel(
 
         last = TILES - 1
 
-        def turn_y(i, name, bufs):
-            xb = bank(name, [P, 2, P], F32, bufs=bufs)
-            words = st["y_bf", i][:].bitcast(F32)
-            for u in range(2):
-                nc.tensor.transpose(xb[:, u, :], words[:, u * P:(u + 1) * P], ident[:])
+        def turn_y(i, name):
+            xb = bank(name, [P, 2, P], F32)
+            turn_pairs(xb, st["y_bf", i][:])
             st["yt", i] = worked("yt", [P, KP], BF16, 4)
             nc.scalar.copy(out=words_of(st["yt", i][:], 1), in_=turned(xb[:]))
 
-        halves = []
-        for g, (name, bufs) in enumerate((("x_geno", 2), ("x_h", 1))):
-            xb = bank(name, [P, 2, P], F32, bufs=bufs)
-            words = st["h", last, g][:].bitcast(F32)
-            for u in range(2):
-                nc.tensor.transpose(xb[:, u, :], words[:, u * P:(u + 1) * P], ident[:])
-            half = worked("g2", [P, KP], BF16)
-            nc.scalar.copy(out=words_of(half[:], 1), in_=turned(xb[:]))
-            halves.append(half)
-        turn_y(last - 2, "x_mix", 1)
+        def round_last():
+            y_bf = worked("y_last", [P, T], BF16)
+            nc.vector.tensor_tensor(
+                out=pair_view(y_bf[:]), in0=pair_order(st["joined", last][:]), in1=pair_order(trait_b[:]), op=ALU.mult
+            )
+            st["y_bf", last] = y_bf
+
+        for g, name in enumerate(("x_h", "x_h1")):
+            xa = bank(name, [P, 2, P], F32)
+            turn_half(last, g, xa)
+            copy_half(last, g, xa[:])
+        turn_y(last - 2, "x_mix")
         join(last - 1)
-        for g in range(G2):
-            codes, scales = quantize(halves[g], "q2", P)
-            st["qh", last, g] = codes[:], scales[:]
-        stage2(last)
+        quantize_half(last, 0)
         finish(last - 1, nc.vector)
+        quantize_half(last, 1)
+        stage2(last)
         round_y(last - 1)
-        join(last)
         quantize_y(last - 2)
-        turn_y(last - 1, "x_geno", 2)
-        y_bf = worked("y_last", [P, T], BF16)
-        nc.vector.tensor_tensor(
-            out=pair_view(y_bf[:]), in0=pair_order(st["joined", last][:]), in1=pair_order(trait_b[:]), op=ALU.mult
-        )
-        st["y_bf", last] = y_bf
-        turn_y(last, "x_mix", 1)
-        finish(last, nc.vector)
+        turn_y(last - 1, "x_geno")
+        join(last)
+        round_last()
+        turn_y(last, "x_mix")
         quantize_y(last - 1)
+        finish(last, nc.vector)
         quantize_y(last)

@@ -17,12 +17,17 @@ ALU = mybir.AluOpType
 
 P = 128
 KP = 512
+PAIRS = KP // 2
 G1 = N // KP
 G2 = E // KP
 JT = J // P
 TILES = C * JT
-UNSORTED = 3
-SORTED = 3
+LAST = TILES - 1
+VAR_COLS = E // P
+TRAIT_COLS = T // P
+SPREAD = 2 * P
+FIRST_SORTED = 3
+Y_BUFS = 10
 
 
 def tile_grouped_association_scores_k7_kernel(
@@ -33,31 +38,31 @@ def tile_grouped_association_scores_k7_kernel(
     with ExitStack() as ctx:
         keep = ctx.enter_context(tc.tile_pool(name="keep", bufs=1))
         work = ctx.enter_context(tc.tile_pool(name="work", bufs=2))
-        ypool = ctx.enter_context(tc.tile_pool(name="ypool", bufs=10))
+        ypool = ctx.enter_context(tc.tile_pool(name="ypool", bufs=Y_BUFS))
         psum = ctx.enter_context(tc.psum_pool(name="psum", bufs=1))
         ctx.enter_context(tc.manual_schedule())
 
         def kept(name, shape, dtype):
-            return keep.tile(shape, dtype, name=name, tag=name, align_bytes=64)
+            return keep.tile(shape, dtype, name=name, tag=name, align_bytes=256)
 
         def worked(name, shape, dtype, bufs=2):
-            return work.tile(shape, dtype, name=name, tag=name, align_bytes=64, bufs=bufs)
+            return work.tile(shape, dtype, name=name, tag=name, align_bytes=256, bufs=bufs)
 
-        def bank(name, shape, dtype, bufs=1):
-            return psum.tile(shape, dtype, name=name, tag=name, bufs=bufs)
+        def bank(name, shape, dtype):
+            return psum.tile(shape, dtype, name=name, tag=name, bufs=1)
 
         ident = kept("ident", [P, P], F32)
         ident_bf = kept("ident_bf", [P, P], BF16)
         var_rows = kept("var_rows", [P, P], BF16)
         gain_rows = kept("gain_rows", [P, P], BF16)
         noise = kept("noise", [P, C], BF16)
-        total_var = kept("total_var", [P, C, 8], F32)
-        inv_var = kept("inv_var", [P, C * 8], F32)
-        gains = kept("gains", [P, TILES + 4], F32)
+        total_var = kept("total_var", [P, C, VAR_COLS], F32)
+        inv_var = kept("inv_var", [P, C * VAR_COLS], F32)
+        gains = kept("gains", [P, TILES + TRAIT_COLS], F32)
         trait_b = kept("trait_b", [P, T], F32)
-        inv_b = [[kept("inv_b%d_%d" % (c, g), [P, KP], F32) for g in range(G2)] for c in range(C)]
+        inv_b = [[kept("inv_b%d_%d" % (c, h), [P, KP], F32) for h in range(G2)] for c in range(C)]
         geno_sb = [kept("geno%d" % i, [P, N], BF16) for i in range(TILES)]
-        u_sb = [[kept("u%d_%d" % (c, h), [P, G1, E], U8) for h in range(G2)] for c in range(C)]
+        u_sb = [[kept("u%d_%d" % (c, h), [P, G1, 2 * KP], U8) for h in range(G2)] for c in range(C)]
         t_sb = [kept("t%d" % c, [P, G2, 2 * T], U8) for c in range(C)]
         z_sb = [kept("z%d" % c, [P, JT, T], BF16) for c in range(C)]
         u_sc = [kept("u_sc%d" % c, [P, G1, E], U8) for c in range(C)]
@@ -65,40 +70,37 @@ def tile_grouped_association_scores_k7_kernel(
         y_codes = [kept("y_codes%d" % c, [P, J], U32) for c in range(C)]
         y_sc = kept("y_sc", [P, J], U8)
 
-        def zero(tile_ap):
+
+        def zero_scales(tile_ap):
             nc.vector.memset(tile_ap.rearrange("p g n -> p (g n)").bitcast(I32), 0)
 
         make_identity(nc, ident[:])
         nc.vector.memset(var_rows[:], 0.0)
-        zero(u_sc[0][:])
+        zero_scales(u_sc[0][:])
         nc.vector.tensor_copy(out=ident_bf[:], in_=ident[:])
-        zero(t_sc[0][:])
+        zero_scales(t_sc[0][:])
         nc.vector.memset(gain_rows[:], 0.0)
         for c in range(1, C):
-            zero(u_sc[c][:])
-            zero(t_sc[c][:])
+            zero_scales(u_sc[c][:])
+            zero_scales(t_sc[c][:])
 
         def load_geno(i):
             c, jt = divmod(i, JT)
             nc.sync.dma_start(out=geno_sb[i][:], in_=geno[c, jt * P:(jt + 1) * P, :])
 
-        def load_words(dst, words, first, count):
-            nc.sync.dma_start(
-                out=dst[:].bitcast(I32),
-                in_=words[first:first + count].rearrange("g p n -> p g n").bitcast(I32),
-            )
-
         def load_u(c, h):
-            nc.sync.dma_start(
-                out=u_sb[c][h][:].bitcast(I32),
-                in_=u_words[c * G1:(c + 1) * G1, :, h * E:(h + 1) * E].rearrange("g p n -> p g n").bitcast(I32),
-            )
+            words = u_words[c * G1:(c + 1) * G1, :, 2 * h * KP:2 * (h + 1) * KP]
+            nc.sync.dma_start(out=u_sb[c][h][:].bitcast(I32), in_=words.rearrange("g p n -> p g n").bitcast(I32))
 
-        def load_scales(dst, scales, first, count):
-            for q in range(4):
+        def load_t(c):
+            words = t_words[c * G2:(c + 1) * G2]
+            nc.sync.dma_start(out=t_sb[c][:].bitcast(I32), in_=words.rearrange("g p n -> p g n").bitcast(I32))
+
+        def load_scales(dst, scales, c, passes):
+            for quad in range(4):
+                rows = scales[c * passes:(c + 1) * passes, 4 * quad:4 * quad + 4, :]
                 nc.sync.dma_start(
-                    out=dst[32 * q:32 * q + 4].bitcast(I32),
-                    in_=scales[first:first + count, 4 * q:4 * q + 4, :].rearrange("g r n -> r g n").bitcast(I32),
+                    out=dst[32 * quad:32 * quad + 4].bitcast(I32), in_=rows.rearrange("g r n -> r g n").bitcast(I32)
                 )
 
         def load_z(c):
@@ -106,100 +108,73 @@ def tile_grouped_association_scores_k7_kernel(
 
         load_geno(0)
         nc.scalar.dma_start(out=noise[:], in_=noise_var.partition_broadcast(P))
-        nc.scalar.dma_start(out=var_rows[0:C * 8, :], in_=comp_var.rearrange("c (b n) -> (c b) n", n=P))
+        nc.scalar.dma_start(out=var_rows[0:C * VAR_COLS, :], in_=comp_var.rearrange("c (b n) -> (c b) n", n=P))
         load_u(0, 0)
         load_scales(u_sc[0], u_scales, 0, G1)
         load_geno(1)
         load_u(0, 1)
         load_geno(2)
         nc.sync.dma_start(out=gain_rows[0:TILES, :], in_=snp_scale.rearrange("c (b n) -> (c b) n", n=P))
-        nc.sync.dma_start(out=gain_rows[TILES:TILES + 4, :], in_=trait_scale.rearrange("(b n) -> b n", n=P))
+        nc.sync.dma_start(
+            out=gain_rows[TILES:TILES + TRAIT_COLS, :], in_=trait_scale.rearrange("(b n) -> b n", n=P)
+        )
         load_geno(3)
-        load_words(t_sb[0], t_words, 0, G2)
+        load_t(0)
         load_scales(t_sc[0], t_scales, 0, G2)
         for c in range(1, C):
             load_geno(c * JT)
             load_z(c - 1)
             load_geno(c * JT + 1)
-            load_scales(u_sc[c], u_scales, c * G1, G1)
-            load_scales(t_sc[c], t_scales, c * G2, G2)
+            load_scales(u_sc[c], u_scales, c, G1)
+            load_scales(t_sc[c], t_scales, c, G2)
             load_u(c, 0)
             load_u(c, 1)
             load_geno(c * JT + 2)
-            load_words(t_sb[c], t_words, c * G2, G2)
+            load_t(c)
             load_geno(c * JT + 3)
         load_z(C - 1)
 
-        st = {}
+
+        def read_in_pair_order(ap):
+            return ap.rearrange("p (m u i) -> p u m i", u=2, i=2)
+
+        def stored_in_pair_order(ap):
+            return ap.rearrange("p (u m i) -> p u m i", u=2, i=2)
+
+        def as_it_lies(ap):
+            return ap
+
+        made = {}
 
         def live(i):
             return 0 <= i < TILES
 
-        def u_scale(c, g, h):
-            return u_sc[c][:, g, h * KP:(h + 1) * KP]
 
-        def sort_view(dst, src):
-            return (
-                dst.rearrange("p (u b k) -> p b u k", u=2, k=4),
-                src.rearrange("p (b k u) -> p b u k", u=2, k=4),
+        def turn_pairs(dst, src):
+            pairs = src.bitcast(F32)
+            for u in range(2):
+                nc.tensor.transpose(dst[:, u, :], pairs[:, u * P:(u + 1) * P], ident[:])
+
+        def copy_turned(dst, src, passes):
+            nc.scalar.copy(
+                out=dst.bitcast(F32).rearrange("p (g j u) -> p g j u", g=passes, u=2),
+                in_=src.rearrange("p (g u) j -> p g j u", u=2),
             )
 
-        def sort_geno(i):
-            st["sorted", i] = worked("sorted", [P, SORTED * 256], F32)
-            dst, src = sort_view(st["sorted", i][:], geno_sb[i][:].bitcast(F32)[:, 0:SORTED * 256])
-            nc.scalar.copy(out=dst, in_=src)
+        def quantize(src, name, width, bufs=2):
+            codes = worked(name + "_codes", [P, width], U32, bufs)
+            scales = worked(name + "_sc", [P, width], U8, bufs)
+            nc.vector.quantize_mx(out=codes[:].bitcast(FP8X4), scales=scales[:], in_=src[:])
+            return [(codes[:, n:n + P], scales[:, n:n + P]) for n in range(0, width, P)]
 
-        def turn_geno(i, g, dst):
-            for u in range(2):
-                if i < UNSORTED or g >= SORTED:
-                    src = geno_sb[i][:].bitcast(F32)[:, 256 * g + u:256 * (g + 1):2]
-                else:
-                    first = P * (SORTED * u + g)
-                    src = st["sorted", i][:, first:first + P]
-                nc.tensor.transpose(dst[:, u, :], src, ident[:])
-
-        def spread_turn(jobs, name="x_spread"):
-            xb = bank(name, [P, 4, P], F32)
-            for k, (cols, first, dst, order) in enumerate(jobs):
-                for b in range(2):
-                    nc.tensor.transpose(
-                        xb[:, 2 * k + b, :], cols[:, first + b:first + b + 1].to_broadcast([P, P]), ident[:]
-                    )
-            return xb
-
-        def spread_copy(jobs, xb):
-            for k, (cols, first, dst, order) in enumerate(jobs):
-                src = xb[:, 2 * k:2 * k + 2, :].rearrange("p b n -> p (b n)")
-                nc.scalar.copy(out=dst, in_=order(src))
-
-        def pair_order(ap):
-            return ap.rearrange("p (m u i) -> p u m i", u=2, i=2)
-
-        def pair_view(ap):
-            return ap.rearrange("p (u m i) -> p u m i", u=2, i=2)
-
-        def inv_job(c, k):
-            g, half = divmod(k, 2)
-            return inv_var, c * 8 + 2 * k, pair_view(inv_b[c][g][:])[:, :, 64 * half:64 * (half + 1), :], pair_order
-
-        def trait_job(k):
-            return gains, TILES + 2 * k, trait_b[:, 256 * k:256 * (k + 1)], lambda ap: ap
-
-        def spread_jobs(s):
-            if s == 3 or s == 4:
-                return [inv_job(1, 2 * s - 6), inv_job(1, 2 * s - 5)]
-            if s == 2:
-                return [trait_job(0), trait_job(1)]
-            c, k = divmod(s + 3, JT)
-            return [inv_job(c, k)] if c < C else []
 
         def make_inv_var():
             xb = bank("x_spread", [P, P], BF16)
             nc.tensor.transpose(xb[:], var_rows[:], ident_bf[:])
             nc.vector.tensor_tensor(
                 out=total_var[:],
-                in0=xb[:, 0:C * 8].rearrange("p (c b) -> p c b", b=8),
-                in1=noise[:].unsqueeze(2).to_broadcast([P, C, 8]),
+                in0=xb[:, 0:C * VAR_COLS].rearrange("p (c b) -> p c b", b=VAR_COLS),
+                in1=noise[:].unsqueeze(2).to_broadcast([P, C, VAR_COLS]),
                 op=ALU.add,
             )
             nc.vector.reciprocal(out=inv_var[:], in_=total_var[:].rearrange("p c b -> p (c b)"))
@@ -207,136 +182,175 @@ def tile_grouped_association_scores_k7_kernel(
         def make_gains():
             xb = bank("x_spread", [P, P], BF16)
             nc.tensor.transpose(xb[:], gain_rows[:], ident_bf[:])
-            nc.scalar.copy(out=gains[:], in_=xb[:, 0:TILES + 4])
+            nc.scalar.copy(out=gains[:], in_=xb[:, 0:TILES + TRAIT_COLS])
 
-        def quantize(src, name, width, bufs=2):
-            codes = worked(name + "_codes", [P, width], U32, bufs)
-            scales = worked(name + "_sc", [P, width], U8, bufs)
-            nc.vector.quantize_mx(out=codes[:].bitcast(FP8X4), scales=scales[:], in_=src[:])
-            return codes, scales
+        def inv_job(c, part):
+            h, half = divmod(part, 2)
+            col = c * VAR_COLS + 2 * part
+            dst = stored_in_pair_order(inv_b[c][h][:])[:, :, half * P // 2:(half + 1) * P // 2, :]
+            return inv_var[:, col:col + 2], dst, read_in_pair_order
 
-        def words_of(tile_ap, groups):
-            return tile_ap.bitcast(F32).rearrange("p (g j u) -> p g j u", g=groups, u=2)
+        def trait_job(part):
+            col = TILES + 2 * part
+            return gains[:, col:col + 2], trait_b[:, part * SPREAD:(part + 1) * SPREAD], as_it_lies
 
-        def turned(bank_ap):
-            return bank_ap.rearrange("p (g u) j -> p g j u", u=2)
+        def spread_jobs(s):
+            if s == 2:
+                return [trait_job(0), trait_job(1)]
+            if s <= 4:
+                return [inv_job(1, 2 * (s - 3)), inv_job(1, 2 * (s - 3) + 1)]
+            c, part = divmod(s + 3, JT)
+            return [inv_job(c, part)] if c < C else []
 
-        def turn_pairs(dst, tile_ap):
-            words = tile_ap.bitcast(F32)
-            for u in range(2):
-                nc.tensor.transpose(dst[:, u, :], words[:, u * P:(u + 1) * P], ident[:])
+        def turn_spread(jobs, name):
+            xb = bank(name, [P, 4, P], F32)
+            for n, (cols, dst, order) in enumerate(jobs):
+                for b in range(2):
+                    nc.tensor.transpose(xb[:, 2 * n + b, :], cols[:, b:b + 1].to_broadcast([P, P]), ident[:])
+            return xb
 
-        def turn_g01(i):
-            if live(i):
-                xb = st["x01", i] = bank("x_geno", [P, 4, P], F32)
-                turn_geno(i, 0, xb[:, 0:2, :])
-                turn_geno(i, 1, xb[:, 2:4, :])
+        def copy_spread(jobs, xb):
+            for n, (cols, dst, order) in enumerate(jobs):
+                nc.scalar.copy(out=dst, in_=order(xb[:, 2 * n:2 * n + 2, :].rearrange("p b n -> p (b n)")))
 
-        def copy_g01(i):
-            if live(i):
-                st["g01", i] = worked("g01", [P, 2 * KP], BF16)
-                nc.scalar.copy(out=words_of(st["g01", i][:], 2), in_=turned(st["x01", i][:]))
 
-        def turn_mix(gi, yi):
-            xb = st["xmix"] = bank("x_mix", [P, 4, P], F32)
-            if live(gi):
-                turn_geno(gi, 2, xb[:, 0:2, :])
-            if live(yi):
-                turn_pairs(xb[:, 2:4, :], st["y_bf", yi][:])
-
-        def copy_mix(gi, yi):
-            lo, hi = (0 if live(gi) else 1), (2 if live(yi) else 1)
-            mix = worked("mix", [P, 2, KP], BF16)
+        def sort_geno(i):
+            made["sorted", i] = worked("sorted", [P, G1 * PAIRS], F32)
             nc.scalar.copy(
-                out=words_of(mix[:, lo:hi, :].rearrange("p g n -> p (g n)"), hi - lo),
-                in_=turned(st["xmix"][:, 2 * lo:2 * hi, :]),
+                out=made["sorted", i][:].rearrange("p (u b k) -> p b u k", u=2, k=4),
+                in_=geno_sb[i][:].bitcast(F32).rearrange("p (b k u) -> p b u k", u=2, k=4),
             )
-            st["g2", gi] = mix[:, 0, :]
-            st["yt", yi] = mix[:, 1, :]
 
-        def turn_h(i):
-            xb = st["xh", i] = bank("x_h", [P, 4, P], F32)
-            for g in range(G2):
-                turn_pairs(xb[:, 2 * g:2 * g + 2, :], st["h", i, g][:])
+        def turn_geno(i, g, dst):
+            for u in range(2):
+                if i < FIRST_SORTED:
+                    src = geno_sb[i][:].bitcast(F32)[:, PAIRS * g + u:PAIRS * (g + 1):2]
+                else:
+                    src = made["sorted", i][:, P * (G1 * u + g):P * (G1 * u + g + 1)]
+                nc.tensor.transpose(dst[:, u, :], src, ident[:])
 
-        def copy_h(i):
-            st["ht", i] = worked("ht", [P, 2 * KP], BF16)
-            nc.scalar.copy(out=words_of(st["ht", i][:], 2), in_=turned(st["xh", i][:]))
+        def turn_geno01(i):
+            xb = made["x01", i] = bank("x_geno", [P, 4, P], F32)
+            turn_geno(i, 0, xb[:, 0:2, :])
+            turn_geno(i, 1, xb[:, 2:4, :])
 
-        def quantize_h(i):
-            codes, scales = quantize(st["ht", i], "qh", 2 * P)
-            for g in range(G2):
-                st["qh", i, g] = codes[:, g * P:(g + 1) * P], scales[:, g * P:(g + 1) * P]
+        def copy_geno01(i):
+            made["g01", i] = worked("g01", [P, 2 * KP], BF16)
+            copy_turned(made["g01", i][:], made["x01", i][:], 2)
 
-        def quantize_g01(i):
-            codes, scales = quantize(st["g01", i], "q01", 2 * P)
-            for g in range(2):
-                st["qg", i, g] = codes[:, g * P:(g + 1) * P], scales[:, g * P:(g + 1) * P]
+        def turn_mix(geno_tile, y_tile):
+            xb = made["xmix"] = bank("x_mix", [P, 4, P], F32)
+            if live(geno_tile):
+                turn_geno(geno_tile, 2, xb[:, 0:2, :])
+            if live(y_tile):
+                turn_pairs(xb[:, 2:4, :], made["y_bf", y_tile][:])
 
-        def quantize_g2(i):
-            codes, scales = quantize(st["g2", i], "q2", P)
-            st["qg", i, 2] = codes[:], scales[:]
+        def copy_mix(geno_tile, y_tile):
+            lo, hi = (0 if live(geno_tile) else 1), (2 if live(y_tile) else 1)
+            mix = worked("mix", [P, 2, KP], BF16)
+            copy_turned(mix[:, lo:hi, :].rearrange("p g n -> p (g n)"), made["xmix"][:, 2 * lo:2 * hi, :], hi - lo)
+            made["g2", geno_tile] = mix[:, 0, :]
+            made["yt", y_tile] = mix[:, 1, :]
+
+        def quantize_geno01(i):
+            made["qg", i, 0], made["qg", i, 1] = quantize(made["g01", i], "q01", 2 * P)
+
+        def quantize_geno2(i):
+            made["qg", i, 2] = quantize(made["g2", i], "q2", P)[0]
+
+
+        def mx_sum(name, stationary, words, scales):
+            acc = bank(name, [P, KP], F32)
+            for g, (codes, code_scales) in enumerate(stationary):
+                nc.tensor.matmul_mx(
+                    out=acc[:],
+                    lhsT=codes.bitcast(FP8X4),
+                    lhsT_scale=code_scales,
+                    rhs=words[:, g, :].bitcast(FP4X4),
+                    rhs_scale=scales[:, g, :],
+                    start=(g == 0),
+                    stop=(g == len(stationary) - 1),
+                )
+            return acc
 
         def stage1(i, h):
             c = i // JT
-            acc = bank("r%d" % h, [P, KP], F32)
-            for g in range(G1):
-                codes, scales = st["qg", i, g]
-                nc.tensor.matmul_mx(
-                    out=acc[:],
-                    lhsT=codes.bitcast(FP8X4),
-                    lhsT_scale=scales,
-                    rhs=u_sb[c][h][:, g, :].bitcast(FP4X4),
-                    rhs_scale=u_scale(c, g, h),
-                    start=(g == 0),
-                    stop=(g == G1 - 1),
-                )
-            st["r", i, h] = acc
+            stationary = [made["qg", i, g] for g in range(G1)]
+            made["r", i, h] = mx_sum("r%d" % h, stationary, u_sb[c][h], u_sc[c][:, :, h * KP:(h + 1) * KP])
 
         def scale_h(i, h):
-            c = i // JT
-            hb = worked("h%d" % h, [P, KP], BF16)
+            made["h", i, h] = worked("h%d" % h, [P, KP], BF16)
             nc.vector.tensor_tensor(
-                out=pair_view(hb[:]), in0=pair_order(st["r", i, h][:]), in1=pair_view(inv_b[c][h][:]), op=ALU.mult
+                out=stored_in_pair_order(made["h", i, h][:]),
+                in0=read_in_pair_order(made["r", i, h][:]),
+                in1=stored_in_pair_order(inv_b[i // JT][h][:]),
+                op=ALU.mult,
             )
-            st["h", i, h] = hb
 
-        def stage2(i, name="d", bufs=1):
+        def turn_h(i, h):
+            xb = made["xh", i, h] = bank(("x_h", "x_h1")[h], [P, 2, P], F32)
+            turn_pairs(xb, made["h", i, h][:])
+
+        def copy_h(i, h):
+            made["ht", i, h] = worked("half%d" % h, [P, KP], BF16)
+            copy_turned(made["ht", i, h][:], made["xh", i, h][:], 1)
+
+        def quantize_h(i, h):
+            made["qh", i, h] = quantize(made["ht", i, h], "qh%d" % h, P)[0]
+
+        def stage2(i):
             c = i // JT
-            acc = bank(name, [P, T], F32, bufs=bufs)
-            for g in range(G2):
-                codes, scales = st["qh", i, g]
-                nc.tensor.matmul_mx(
-                    out=acc[:],
-                    lhsT=codes.bitcast(FP8X4),
-                    lhsT_scale=scales,
-                    rhs=t_sb[c][:, g, :].bitcast(FP4X4),
-                    rhs_scale=t_sc[c][:, g, :],
-                    start=(g == 0),
-                    stop=(g == G2 - 1),
-                )
-            st["d", i] = acc
+            made["d", i] = mx_sum("d", [made["qh", i, h] for h in range(G2)], t_sb[c], t_sc[c])
+
 
         def join(i):
             c, jt = divmod(i, JT)
-            joined = worked("joined", [P, T], F32, 3)
+            made["joined", i] = worked("joined", [P, T], F32, 3)
             nc.vector.scalar_tensor_tensor(
-                out=joined[:], in0=st["d", i][:], scalar=gains[:, i:i + 1], in1=z_sb[c][:, jt, :],
+                out=made["joined", i][:], in0=made["d", i][:], scalar=gains[:, i:i + 1], in1=z_sb[c][:, jt, :],
                 op0=ALU.mult, op1=ALU.add,
             )
-            st["joined", i] = joined
 
-        def finish(i, engine):
+        def finish(i):
             c, jt = divmod(i, JT)
-            y = ypool.tile([P, T], F32, name="y", tag="y", align_bytes=64)
-            engine.tensor_tensor(out=y[:], in0=st["joined", i][:], in1=trait_b[:], op=ALU.mult)
+            y = made["y", i] = ypool.tile([P, T], F32, name="y", tag="y", align_bytes=256)
+            nc.vector.tensor_tensor(out=y[:], in0=made["joined", i][:], in1=trait_b[:], op=ALU.mult)
             nc.sync.dma_start(out=out_0[c, jt * P:(jt + 1) * P, :], in_=y[:])
-            st["y", i] = y
 
         def round_y(i):
-            y_bf = worked("y_bf", [P, T], BF16)
-            nc.scalar.copy(out=pair_view(y_bf[:]), in_=pair_order(st["y", i][:]))
-            st["y_bf", i] = y_bf
+            made["y_bf", i] = worked("y_bf", [P, T], BF16)
+            nc.scalar.copy(out=stored_in_pair_order(made["y_bf", i][:]), in_=read_in_pair_order(made["y", i][:]))
+
+        def last_half(k):
+            return slice(k * T // 2, (k + 1) * T // 2)
+
+        def join_last(k):
+            made["joined", LAST, k] = worked("joined_last%d" % k, [P, T // 2], F32, 1)
+            nc.vector.scalar_tensor_tensor(
+                out=made["joined", LAST, k][:], in0=made["d", LAST][:, last_half(k)], scalar=gains[:, LAST:LAST + 1],
+                in1=z_sb[C - 1][:, JT - 1, last_half(k)], op0=ALU.mult, op1=ALU.add,
+            )
+
+        def round_last(k):
+            nc.vector.tensor_tensor(
+                out=stored_in_pair_order(made["y_bf", LAST][:])[:, :, k * P // 2:(k + 1) * P // 2, :],
+                in0=read_in_pair_order(made["joined", LAST, k][:]),
+                in1=read_in_pair_order(trait_b[:, last_half(k)]),
+                op=ALU.mult,
+            )
+
+        def finish_last(k):
+            y = worked("y_last%d" % k, [P, T // 2], F32, 1)
+            nc.vector.tensor_tensor(
+                out=y[:], in0=made["joined", LAST, k][:], in1=trait_b[:, last_half(k)], op=ALU.mult
+            )
+            nc.sync.dma_start(out=out_0[C - 1, J - P:J, last_half(k)], in_=y[:])
+
+        def turn_and_copy_y(i, name):
+            xb = bank(name, [P, 2, P], F32)
+            turn_pairs(xb, made["y_bf", i][:])
+            made["yt", i] = worked("yt", [P, KP], BF16, 4)
+            copy_turned(made["yt", i][:], xb[:], 1)
 
         words_out = out_1[0].rearrange("p m t -> p (m t)").bitcast(I32)
 
@@ -344,89 +358,74 @@ def tile_grouped_association_scores_k7_kernel(
             c, jt = divmod(i, JT)
             cols = slice(jt * P, (jt + 1) * P)
             nc.vector.quantize_mx(
-                out=y_codes[c][:, cols].bitcast(FP8X4), scales=y_sc[4 * c:P, cols], in_=st["yt", i][:]
+                out=y_codes[c][:, cols].bitcast(FP8X4), scales=y_sc[4 * c:P, cols], in_=made["yt", i][:]
             )
-            first = None
-            if jt == JT - 1:
-                first = 2 if c == C - 1 else 0
-            elif c == C - 1 and jt == 1:
-                first = 0
-            if first is not None:
-                nc.sync.dma_start(
-                    out=words_out[:, c * J + first * P:c * J + (jt + 1) * P],
-                    in_=y_codes[c][:, first * P:(jt + 1) * P].bitcast(I32),
+            if jt == JT - 1 or i == LAST - 1:
+                lo, hi = (jt * P if i == LAST else 0), (jt + 1) * P
+                nc.sync.dma_start(out=words_out[:, c * J + lo:c * J + hi], in_=y_codes[c][:, lo:hi].bitcast(I32))
+
+        def store_y_scales():
+            for quad in range(4):
+                (nc.scalar if quad % 2 == 0 else nc.sync).dma_start(
+                    out=out_2[0, 4 * quad:4 * quad + 4, :].rearrange("r (c j) -> c r j", c=C).bitcast(I32),
+                    in_=y_sc[32 * quad:32 * quad + 4 * C, :].bitcast(I32),
                 )
-            if i == TILES - 1:
-                for q in range(4):
-                    (nc.scalar if q % 2 == 0 else nc.sync).dma_start(
-                        out=out_2[0, 4 * q:4 * q + 4, :].rearrange("r (c j) -> c r j", c=C).bitcast(I32),
-                        in_=y_sc[32 * q:32 * q + 16, :].bitcast(I32),
-                    )
+
 
         make_inv_var()
-        first = []
+        first_passes = []
         for g, name in enumerate(("x_geno", "x_mix", "x_h1")):
-            xa = bank(name, [P, 2, P], F32)
-            turn_geno(0, g, xa)
-            part = worked("first%d" % g, [P, KP], BF16, 1)
-            nc.scalar.copy(out=words_of(part[:], 1), in_=turned(xa[:]))
-            first.append(part)
+            xb = bank(name, [P, 2, P], F32)
+            turn_geno(0, g, xb)
+            first_pass = worked("first%d" % g, [P, KP], BF16, 1)
+            copy_turned(first_pass[:], xb[:], 1)
+            first_passes.append(first_pass)
         for g in range(G1):
-            codes, scales = quantize(first[g], "qfirst%d" % g, P, 1)
-            st["qg", 0, g] = codes[:], scales[:]
-        for g in range(G2):
-            jobs = [inv_job(0, 2 * g), inv_job(0, 2 * g + 1)]
-            spread_copy(jobs, spread_turn(jobs, ("x_spread", "x_h")[g]))
+            made["qg", 0, g] = quantize(first_passes[g], "qfirst%d" % g, P, 1)[0]
+        for h, name in enumerate(("x_spread", "x_h")):
+            jobs = [inv_job(0, 2 * h), inv_job(0, 2 * h + 1)]
+            copy_spread(jobs, turn_spread(jobs, name))
         stage1(0, 0)
         scale_h(0, 0)
-        turn_g01(1)
+        turn_geno01(1)
         turn_mix(1, -1)
-        copy_g01(1)
+        copy_geno01(1)
         copy_mix(1, -1)
         stage1(0, 1)
         scale_h(0, 1)
         make_gains()
-        def turn_half(i, g, dst):
-            turn_pairs(dst, st["h", i, g][:])
-
-        def copy_half(i, g, src):
-            st["half", i, g] = worked("half%d" % g, [P, KP], BF16)
-            nc.scalar.copy(out=words_of(st["half", i, g][:], 1), in_=turned(src))
-
-        def quantize_half(i, g):
-            codes, scales = quantize(st["half", i, g], "qh%d" % g, P)
-            st["qh", i, g] = codes[:], scales[:]
 
         for s in range(2, TILES + 1):
             jobs = spread_jobs(s)
             if live(s + 1):
                 sort_geno(s + 1)
-            quantize_g01(s - 1)
+            quantize_geno01(s - 1)
             if s == TILES:
-                quantize_g2(s - 1)
+                quantize_geno2(s - 1)
             if live(s - 3):
                 join(s - 3)
             if s < TILES:
-                quantize_g2(s - 1)
+                quantize_geno2(s - 1)
             if live(s - 3):
-                finish(s - 3, nc.vector)
-            xa = bank("x_h", [P, 2, P], F32)
-            turn_half(s - 2, 0, xa)
-            turn_g01(s)
+                finish(s - 3)
+            turn_h(s - 2, 0)
+            if live(s):
+                turn_geno01(s)
             turn_mix(s, s - 4)
-            xb = spread_turn(jobs) if jobs else None
-            xc = bank("x_h1", [P, 2, P], F32)
-            turn_half(s - 2, 1, xc)
-            copy_half(s - 2, 0, xa[:])
-            copy_g01(s)
-            copy_half(s - 2, 1, xc[:])
+            if jobs:
+                x_spread = turn_spread(jobs, "x_spread")
+            turn_h(s - 2, 1)
+            copy_h(s - 2, 0)
+            if live(s):
+                copy_geno01(s)
+            copy_h(s - 2, 1)
             copy_mix(s, s - 4)
             if live(s - 3):
                 round_y(s - 3)
             if jobs:
-                spread_copy(jobs, xb)
-            quantize_half(s - 2, 0)
-            quantize_half(s - 2, 1)
+                copy_spread(jobs, x_spread)
+            quantize_h(s - 2, 0)
+            quantize_h(s - 2, 1)
             stage1(s - 1, 0)
             scale_h(s - 1, 0)
             if live(s - 4):
@@ -435,37 +434,25 @@ def tile_grouped_association_scores_k7_kernel(
             scale_h(s - 1, 1)
             stage2(s - 2)
 
-        last = TILES - 1
-
-        def turn_y(i, name):
-            xb = bank(name, [P, 2, P], F32)
-            turn_pairs(xb, st["y_bf", i][:])
-            st["yt", i] = worked("yt", [P, KP], BF16, 4)
-            nc.scalar.copy(out=words_of(st["yt", i][:], 1), in_=turned(xb[:]))
-
-        def round_last():
-            y_bf = worked("y_last", [P, T], BF16)
-            nc.vector.tensor_tensor(
-                out=pair_view(y_bf[:]), in0=pair_order(st["joined", last][:]), in1=pair_order(trait_b[:]), op=ALU.mult
-            )
-            st["y_bf", last] = y_bf
-
-        for g, name in enumerate(("x_h", "x_h1")):
-            xa = bank(name, [P, 2, P], F32)
-            turn_half(last, g, xa)
-            copy_half(last, g, xa[:])
-        turn_y(last - 2, "x_mix")
-        join(last - 1)
-        quantize_half(last, 0)
-        finish(last - 1, nc.vector)
-        quantize_half(last, 1)
-        stage2(last)
-        round_y(last - 1)
-        quantize_y(last - 2)
-        turn_y(last - 1, "x_geno")
-        join(last)
-        round_last()
-        turn_y(last, "x_mix")
-        quantize_y(last - 1)
-        finish(last, nc.vector)
-        quantize_y(last)
+        for h in range(G2):
+            turn_h(LAST, h)
+            copy_h(LAST, h)
+        turn_and_copy_y(LAST - 2, "x_mix")
+        join(LAST - 1)
+        quantize_h(LAST, 0)
+        finish(LAST - 1)
+        quantize_h(LAST, 1)
+        stage2(LAST)
+        round_y(LAST - 1)
+        quantize_y(LAST - 2)
+        turn_and_copy_y(LAST - 1, "x_geno")
+        made["y_bf", LAST] = worked("y_bf_last", [P, T], BF16, 1)
+        for step in (join_last, round_last):
+            for k in range(2):
+                step(k)
+        turn_and_copy_y(LAST, "x_mix")
+        quantize_y(LAST - 1)
+        for k in range(2):
+            finish_last(k)
+        quantize_y(LAST)
+        store_y_scales()

from contextlib import ExitStack

import concourse.mybir as mybir
from concourse.masks import make_identity

C, J, N, E, T = 4, 512, 1536, 1024, 512
FLOPS = 2 * C * J * (N * E + E * T)

F32 = mybir.dt.float32
BF16 = mybir.dt.bfloat16
I32 = mybir.dt.int32
U32 = mybir.dt.uint32
U8 = mybir.dt.uint8
FP8X4 = mybir.dt.float8_e4m3fn_x4
FP4X4 = mybir.dt.float4_e2m1fn_x4
ALU = mybir.AluOpType

P = 128
KP = 512
PAIRS = KP // 2
G1 = N // KP
G2 = E // KP
JT = J // P
TILES = C * JT
LAST = TILES - 1
VAR_COLS = E // P
TRAIT_COLS = T // P
SPREAD = 2 * P
FIRST_SORTED = 3
Y_BUFS = 10


def tile_grouped_association_scores_k7_kernel(
    tc, geno, u_words, u_scales, comp_var, noise_var, t_words, t_scales,
    snp_scale, z_other, trait_scale, out_0, out_1, out_2,
):
    nc = tc.nc
    with ExitStack() as ctx:
        keep = ctx.enter_context(tc.tile_pool(name="keep", bufs=1))
        work = ctx.enter_context(tc.tile_pool(name="work", bufs=2))
        ypool = ctx.enter_context(tc.tile_pool(name="ypool", bufs=Y_BUFS))
        psum = ctx.enter_context(tc.psum_pool(name="psum", bufs=1))
        ctx.enter_context(tc.manual_schedule())

        def kept(name, shape, dtype):
            return keep.tile(shape, dtype, name=name, tag=name, align_bytes=256)

        def worked(name, shape, dtype, bufs=2):
            return work.tile(shape, dtype, name=name, tag=name, align_bytes=256, bufs=bufs)

        def bank(name, shape, dtype):
            return psum.tile(shape, dtype, name=name, tag=name, bufs=1)

        ident = kept("ident", [P, P], F32)
        ident_bf = kept("ident_bf", [P, P], BF16)
        var_rows = kept("var_rows", [P, P], BF16)
        gain_rows = kept("gain_rows", [P, P], BF16)
        noise = kept("noise", [P, C], BF16)
        total_var = kept("total_var", [P, C, VAR_COLS], F32)
        inv_var = kept("inv_var", [P, C * VAR_COLS], F32)
        gains = kept("gains", [P, TILES + TRAIT_COLS], F32)
        trait_b = kept("trait_b", [P, T], F32)
        inv_b = [[kept("inv_b%d_%d" % (c, h), [P, KP], F32) for h in range(G2)] for c in range(C)]
        geno_sb = [kept("geno%d" % i, [P, N], BF16) for i in range(TILES)]
        u_sb = [[kept("u%d_%d" % (c, h), [P, G1, 2 * KP], U8) for h in range(G2)] for c in range(C)]
        t_sb = [kept("t%d" % c, [P, G2, 2 * T], U8) for c in range(C)]
        z_sb = [kept("z%d" % c, [P, JT, T], BF16) for c in range(C)]
        u_sc = [kept("u_sc%d" % c, [P, G1, E], U8) for c in range(C)]
        t_sc = [kept("t_sc%d" % c, [P, G2, T], U8) for c in range(C)]
        y_codes = [kept("y_codes%d" % c, [P, J], U32) for c in range(C)]
        y_sc = kept("y_sc", [P, J], U8)


        def zero_scales(tile_ap):
            nc.vector.memset(tile_ap.rearrange("p g n -> p (g n)").bitcast(I32), 0)

        make_identity(nc, ident[:])
        nc.vector.memset(var_rows[:], 0.0)
        zero_scales(u_sc[0][:])
        nc.vector.tensor_copy(out=ident_bf[:], in_=ident[:])
        zero_scales(t_sc[0][:])
        nc.vector.memset(gain_rows[:], 0.0)
        for c in range(1, C):
            zero_scales(u_sc[c][:])
            zero_scales(t_sc[c][:])

        def load_geno(i):
            c, jt = divmod(i, JT)
            nc.sync.dma_start(out=geno_sb[i][:], in_=geno[c, jt * P:(jt + 1) * P, :])

        def load_u(c, h):
            words = u_words[c * G1:(c + 1) * G1, :, 2 * h * KP:2 * (h + 1) * KP]
            nc.sync.dma_start(out=u_sb[c][h][:].bitcast(I32), in_=words.rearrange("g p n -> p g n").bitcast(I32))

        def load_t(c):
            words = t_words[c * G2:(c + 1) * G2]
            nc.sync.dma_start(out=t_sb[c][:].bitcast(I32), in_=words.rearrange("g p n -> p g n").bitcast(I32))

        def load_scales(dst, scales, c, passes):
            for quad in range(4):
                rows = scales[c * passes:(c + 1) * passes, 4 * quad:4 * quad + 4, :]
                nc.sync.dma_start(
                    out=dst[32 * quad:32 * quad + 4].bitcast(I32), in_=rows.rearrange("g r n -> r g n").bitcast(I32)
                )

        def load_z(c):
            nc.sync.dma_start(out=z_sb[c][:], in_=z_other[c].rearrange("(s p) n -> p s n", p=P))

        load_geno(0)
        nc.scalar.dma_start(out=noise[:], in_=noise_var.partition_broadcast(P))
        nc.scalar.dma_start(out=var_rows[0:C * VAR_COLS, :], in_=comp_var.rearrange("c (b n) -> (c b) n", n=P))
        load_u(0, 0)
        load_scales(u_sc[0], u_scales, 0, G1)
        load_geno(1)
        load_u(0, 1)
        load_geno(2)
        nc.sync.dma_start(out=gain_rows[0:TILES, :], in_=snp_scale.rearrange("c (b n) -> (c b) n", n=P))
        nc.sync.dma_start(
            out=gain_rows[TILES:TILES + TRAIT_COLS, :], in_=trait_scale.rearrange("(b n) -> b n", n=P)
        )
        load_geno(3)
        load_t(0)
        load_scales(t_sc[0], t_scales, 0, G2)
        for c in range(1, C):
            load_geno(c * JT)
            load_z(c - 1)
            load_geno(c * JT + 1)
            load_scales(u_sc[c], u_scales, c, G1)
            load_scales(t_sc[c], t_scales, c, G2)
            load_u(c, 0)
            load_u(c, 1)
            load_geno(c * JT + 2)
            load_t(c)
            load_geno(c * JT + 3)
        load_z(C - 1)


        def read_in_pair_order(ap):
            return ap.rearrange("p (m u i) -> p u m i", u=2, i=2)

        def stored_in_pair_order(ap):
            return ap.rearrange("p (u m i) -> p u m i", u=2, i=2)

        def as_it_lies(ap):
            return ap

        made = {}

        def live(i):
            return 0 <= i < TILES


        def turn_pairs(dst, src):
            pairs = src.bitcast(F32)
            for u in range(2):
                nc.tensor.transpose(dst[:, u, :], pairs[:, u * P:(u + 1) * P], ident[:])

        def copy_turned(dst, src, passes):
            nc.scalar.copy(
                out=dst.bitcast(F32).rearrange("p (g j u) -> p g j u", g=passes, u=2),
                in_=src.rearrange("p (g u) j -> p g j u", u=2),
            )

        def quantize(src, name, width, bufs=2):
            codes = worked(name + "_codes", [P, width], U32, bufs)
            scales = worked(name + "_sc", [P, width], U8, bufs)
            nc.vector.quantize_mx(out=codes[:].bitcast(FP8X4), scales=scales[:], in_=src[:])
            return [(codes[:, n:n + P], scales[:, n:n + P]) for n in range(0, width, P)]


        def make_inv_var():
            xb = bank("x_spread", [P, P], BF16)
            nc.tensor.transpose(xb[:], var_rows[:], ident_bf[:])
            nc.vector.tensor_tensor(
                out=total_var[:],
                in0=xb[:, 0:C * VAR_COLS].rearrange("p (c b) -> p c b", b=VAR_COLS),
                in1=noise[:].unsqueeze(2).to_broadcast([P, C, VAR_COLS]),
                op=ALU.add,
            )
            nc.vector.reciprocal(out=inv_var[:], in_=total_var[:].rearrange("p c b -> p (c b)"))

        def make_gains():
            xb = bank("x_spread", [P, P], BF16)
            nc.tensor.transpose(xb[:], gain_rows[:], ident_bf[:])
            nc.scalar.copy(out=gains[:], in_=xb[:, 0:TILES + TRAIT_COLS])

        def inv_job(c, part):
            h, half = divmod(part, 2)
            col = c * VAR_COLS + 2 * part
            dst = stored_in_pair_order(inv_b[c][h][:])[:, :, half * P // 2:(half + 1) * P // 2, :]
            return inv_var[:, col:col + 2], dst, read_in_pair_order

        def trait_job(part):
            col = TILES + 2 * part
            return gains[:, col:col + 2], trait_b[:, part * SPREAD:(part + 1) * SPREAD], as_it_lies

        def spread_jobs(s):
            if s == 2:
                return [trait_job(0), trait_job(1)]
            if s <= 4:
                return [inv_job(1, 2 * (s - 3)), inv_job(1, 2 * (s - 3) + 1)]
            c, part = divmod(s + 3, JT)
            return [inv_job(c, part)] if c < C else []

        def turn_spread(jobs, name):
            xb = bank(name, [P, 4, P], F32)
            for n, (cols, dst, order) in enumerate(jobs):
                for b in range(2):
                    nc.tensor.transpose(xb[:, 2 * n + b, :], cols[:, b:b + 1].to_broadcast([P, P]), ident[:])
            return xb

        def copy_spread(jobs, xb):
            for n, (cols, dst, order) in enumerate(jobs):
                nc.scalar.copy(out=dst, in_=order(xb[:, 2 * n:2 * n + 2, :].rearrange("p b n -> p (b n)")))


        def sort_geno(i):
            made["sorted", i] = worked("sorted", [P, G1 * PAIRS], F32)
            nc.scalar.copy(
                out=made["sorted", i][:].rearrange("p (u b k) -> p b u k", u=2, k=4),
                in_=geno_sb[i][:].bitcast(F32).rearrange("p (b k u) -> p b u k", u=2, k=4),
            )

        def turn_geno(i, g, dst):
            for u in range(2):
                if i < FIRST_SORTED:
                    src = geno_sb[i][:].bitcast(F32)[:, PAIRS * g + u:PAIRS * (g + 1):2]
                else:
                    src = made["sorted", i][:, P * (G1 * u + g):P * (G1 * u + g + 1)]
                nc.tensor.transpose(dst[:, u, :], src, ident[:])

        def turn_geno01(i):
            xb = made["x01", i] = bank("x_geno", [P, 4, P], F32)
            turn_geno(i, 0, xb[:, 0:2, :])
            turn_geno(i, 1, xb[:, 2:4, :])

        def copy_geno01(i):
            made["g01", i] = worked("g01", [P, 2 * KP], BF16)
            copy_turned(made["g01", i][:], made["x01", i][:], 2)

        def turn_mix(geno_tile, y_tile):
            xb = made["xmix"] = bank("x_mix", [P, 4, P], F32)
            if live(geno_tile):
                turn_geno(geno_tile, 2, xb[:, 0:2, :])
            if live(y_tile):
                turn_pairs(xb[:, 2:4, :], made["y_bf", y_tile][:])

        def copy_mix(geno_tile, y_tile):
            lo, hi = (0 if live(geno_tile) else 1), (2 if live(y_tile) else 1)
            mix = worked("mix", [P, 2, KP], BF16)
            copy_turned(mix[:, lo:hi, :].rearrange("p g n -> p (g n)"), made["xmix"][:, 2 * lo:2 * hi, :], hi - lo)
            made["g2", geno_tile] = mix[:, 0, :]
            made["yt", y_tile] = mix[:, 1, :]

        def quantize_geno01(i):
            made["qg", i, 0], made["qg", i, 1] = quantize(made["g01", i], "q01", 2 * P)

        def quantize_geno2(i):
            made["qg", i, 2] = quantize(made["g2", i], "q2", P)[0]


        def mx_sum(name, stationary, words, scales):
            acc = bank(name, [P, KP], F32)
            for g, (codes, code_scales) in enumerate(stationary):
                nc.tensor.matmul_mx(
                    out=acc[:],
                    lhsT=codes.bitcast(FP8X4),
                    lhsT_scale=code_scales,
                    rhs=words[:, g, :].bitcast(FP4X4),
                    rhs_scale=scales[:, g, :],
                    start=(g == 0),
                    stop=(g == len(stationary) - 1),
                )
            return acc

        def stage1(i, h):
            c = i // JT
            stationary = [made["qg", i, g] for g in range(G1)]
            made["r", i, h] = mx_sum("r%d" % h, stationary, u_sb[c][h], u_sc[c][:, :, h * KP:(h + 1) * KP])

        def scale_h(i, h):
            made["h", i, h] = worked("h%d" % h, [P, KP], BF16)
            nc.vector.tensor_tensor(
                out=stored_in_pair_order(made["h", i, h][:]),
                in0=read_in_pair_order(made["r", i, h][:]),
                in1=stored_in_pair_order(inv_b[i // JT][h][:]),
                op=ALU.mult,
            )

        def turn_h(i, h):
            xb = made["xh", i, h] = bank(("x_h", "x_h1")[h], [P, 2, P], F32)
            turn_pairs(xb, made["h", i, h][:])

        def copy_h(i, h):
            made["ht", i, h] = worked("half%d" % h, [P, KP], BF16)
            copy_turned(made["ht", i, h][:], made["xh", i, h][:], 1)

        def quantize_h(i, h):
            made["qh", i, h] = quantize(made["ht", i, h], "qh%d" % h, P)[0]

        def stage2(i):
            c = i // JT
            made["d", i] = mx_sum("d", [made["qh", i, h] for h in range(G2)], t_sb[c], t_sc[c])


        def join(i):
            c, jt = divmod(i, JT)
            made["joined", i] = worked("joined", [P, T], F32, 3)
            nc.vector.scalar_tensor_tensor(
                out=made["joined", i][:], in0=made["d", i][:], scalar=gains[:, i:i + 1], in1=z_sb[c][:, jt, :],
                op0=ALU.mult, op1=ALU.add,
            )

        def finish(i):
            c, jt = divmod(i, JT)
            y = made["y", i] = ypool.tile([P, T], F32, name="y", tag="y", align_bytes=256)
            nc.vector.tensor_tensor(out=y[:], in0=made["joined", i][:], in1=trait_b[:], op=ALU.mult)
            nc.sync.dma_start(out=out_0[c, jt * P:(jt + 1) * P, :], in_=y[:])

        def round_y(i):
            made["y_bf", i] = worked("y_bf", [P, T], BF16)
            nc.scalar.copy(out=stored_in_pair_order(made["y_bf", i][:]), in_=read_in_pair_order(made["y", i][:]))

        def last_half(k):
            return slice(k * T // 2, (k + 1) * T // 2)

        def join_last(k):
            made["joined", LAST, k] = worked("joined_last%d" % k, [P, T // 2], F32, 1)
            nc.vector.scalar_tensor_tensor(
                out=made["joined", LAST, k][:], in0=made["d", LAST][:, last_half(k)], scalar=gains[:, LAST:LAST + 1],
                in1=z_sb[C - 1][:, JT - 1, last_half(k)], op0=ALU.mult, op1=ALU.add,
            )

        def round_last(k):
            nc.vector.tensor_tensor(
                out=stored_in_pair_order(made["y_bf", LAST][:])[:, :, k * P // 2:(k + 1) * P // 2, :],
                in0=read_in_pair_order(made["joined", LAST, k][:]),
                in1=read_in_pair_order(trait_b[:, last_half(k)]),
                op=ALU.mult,
            )

        def finish_last(k):
            y = worked("y_last%d" % k, [P, T // 2], F32, 1)
            nc.vector.tensor_tensor(
                out=y[:], in0=made["joined", LAST, k][:], in1=trait_b[:, last_half(k)], op=ALU.mult
            )
            nc.sync.dma_start(out=out_0[C - 1, J - P:J, last_half(k)], in_=y[:])

        def turn_and_copy_y(i, name):
            xb = bank(name, [P, 2, P], F32)
            turn_pairs(xb, made["y_bf", i][:])
            made["yt", i] = worked("yt", [P, KP], BF16, 4)
            copy_turned(made["yt", i][:], xb[:], 1)

        words_out = out_1[0].rearrange("p m t -> p (m t)").bitcast(I32)

        def quantize_y(i):
            c, jt = divmod(i, JT)
            cols = slice(jt * P, (jt + 1) * P)
            nc.vector.quantize_mx(
                out=y_codes[c][:, cols].bitcast(FP8X4), scales=y_sc[4 * c:P, cols], in_=made["yt", i][:]
            )
            if jt == JT - 1 or i == LAST - 1:
                lo, hi = (jt * P if i == LAST else 0), (jt + 1) * P
                nc.sync.dma_start(out=words_out[:, c * J + lo:c * J + hi], in_=y_codes[c][:, lo:hi].bitcast(I32))

        def store_y_scales():
            for quad in range(4):
                (nc.scalar if quad % 2 == 0 else nc.sync).dma_start(
                    out=out_2[0, 4 * quad:4 * quad + 4, :].rearrange("r (c j) -> c r j", c=C).bitcast(I32),
                    in_=y_sc[32 * quad:32 * quad + 4 * C, :].bitcast(I32),
                )


        make_inv_var()
        first_passes = []
        for g, name in enumerate(("x_geno", "x_mix", "x_h1")):
            xb = bank(name, [P, 2, P], F32)
            turn_geno(0, g, xb)
            first_pass = worked("first%d" % g, [P, KP], BF16, 1)
            copy_turned(first_pass[:], xb[:], 1)
            first_passes.append(first_pass)
        for g in range(G1):
            made["qg", 0, g] = quantize(first_passes[g], "qfirst%d" % g, P, 1)[0]
        for h, name in enumerate(("x_spread", "x_h")):
            jobs = [inv_job(0, 2 * h), inv_job(0, 2 * h + 1)]
            copy_spread(jobs, turn_spread(jobs, name))
        stage1(0, 0)
        scale_h(0, 0)
        turn_geno01(1)
        turn_mix(1, -1)
        copy_geno01(1)
        copy_mix(1, -1)
        stage1(0, 1)
        scale_h(0, 1)
        make_gains()

        for s in range(2, TILES + 1):
            jobs = spread_jobs(s)
            if live(s + 1):
                sort_geno(s + 1)
            quantize_geno01(s - 1)
            if s == TILES:
                quantize_geno2(s - 1)
            if live(s - 3):
                join(s - 3)
            if s < TILES:
                quantize_geno2(s - 1)
            if live(s - 3):
                finish(s - 3)
            turn_h(s - 2, 0)
            if live(s):
                turn_geno01(s)
            turn_mix(s, s - 4)
            if jobs:
                x_spread = turn_spread(jobs, "x_spread")
            turn_h(s - 2, 1)
            copy_h(s - 2, 0)
            if live(s):
                copy_geno01(s)
            copy_h(s - 2, 1)
            copy_mix(s, s - 4)
            if live(s - 3):
                round_y(s - 3)
            if jobs:
                copy_spread(jobs, x_spread)
            quantize_h(s - 2, 0)
            quantize_h(s - 2, 1)
            stage1(s - 1, 0)
            scale_h(s - 1, 0)
            if live(s - 4):
                quantize_y(s - 4)
            stage1(s - 1, 1)
            scale_h(s - 1, 1)
            stage2(s - 2)

        for h in range(G2):
            turn_h(LAST, h)
            copy_h(LAST, h)
        turn_and_copy_y(LAST - 2, "x_mix")
        join(LAST - 1)
        quantize_h(LAST, 0)
        finish(LAST - 1)
        quantize_h(LAST, 1)
        stage2(LAST)
        round_y(LAST - 1)
        quantize_y(LAST - 2)
        turn_and_copy_y(LAST - 1, "x_geno")
        made["y_bf", LAST] = worked("y_bf_last", [P, T], BF16, 1)
        for step in (join_last, round_last):
            for k in range(2):
                step(k)
        turn_and_copy_y(LAST, "x_mix")
        quantize_y(LAST - 1)
        for k in range(2):
            finish_last(k)
        quantize_y(LAST)
        store_y_scales()
